import numpy as np, ml_dtypes
CORES = [16,17,18,19,32,33,34,35]
N = 8
BF = ml_dtypes.bfloat16
def gentries(a):
    return np.ascontiguousarray(a.reshape(8, 16, -1).transpose(0, 2, 1)).reshape(8, -1)
def gtable(e):
    e = np.asarray(e); return np.ascontiguousarray(e.reshape(8, -1, 16).transpose(0, 2, 1)).reshape(128, -1).astype(np.int32)
NO, D, B, K, RO, TH = 20, 4, 160, 8, 5, 9
V, NB = NO * B, NO + D
def every(z):
    return np.concatenate([z, np.stack([np.roll(z[:, :, d - 1], d, axis=0) for d in range(1, D + 1)], axis=2)], axis=2)
def parts(rng):
    a = rng.integers(0, 256, (N, 8, 15, V)); m = (rng.random((N, 8, V)) < 0.0625).astype(np.int64)
    u = np.argsort(rng.random((N, 8, NB, V)), axis=-1)[..., :16 * B].reshape(N, 8, NB, 16, B)
    e = np.argsort(rng.random((N, 8, NO, B)), axis=-1)[..., :K]
    return a, m, u, np.ascontiguousarray(e)
def firsts(e):
    z = np.zeros((N, 8, V), bool); np.put_along_axis(z, (e + B * np.arange(NO)[:, None]).reshape(N, 8, -1), True, 2)
    return z
def reach(u, e):
    z = np.zeros((N, 8, V), bool); q = np.take_along_axis(u, every(e)[:, :, :, None, :], 4)
    np.put_along_axis(z, q.reshape(N, 8, -1), True, 2)
    return z
def cover(rng):
    o = np.argsort(rng.random((N, V)), axis=-1)
    return np.stack([np.roll(o, -16 * K * c, axis=1) for c in range(NB)], axis=1)
def aim(rng, e, g, o):
    ee = every(e)[:, g]; w = np.zeros((N, NB, 16, B), np.int64)
    for r in range(N):
        for c in range(NB):
            rest = np.ones(B, bool); rest[ee[r, c]] = False
            w[r, c][:, ee[r, c]] = o[r, c, :16 * K].reshape(16, K)
            w[r, c][:, rest] = rng.permutation(o[r, c, 16 * K:])[:16 * (B - K)].reshape(16, B - K)
    return w
def pack(a, m, u, e):
    rec = np.concatenate([a, m[:, :, None]], axis=2).reshape(N, 128, V).astype(np.float32).astype(BF)
    up = np.ascontiguousarray(u.transpose(0, 1, 3, 2, 4).reshape(N, 128, NB * B)).astype(np.int32)
    return {"rec": rec, "up": up, "fr": np.stack([gtable(z.reshape(8, -1)) for z in e])}
def setup_inputs(rng):
    return pack(*parts(rng))
def setup_inputs_room(rng):
    a, m, u, e = parts(rng); c = reach(u, e); z = firsts(e); can = c & ~z; pick = np.zeros((N, 8, V), bool)
    for r in range(N):
        for g in range(8):
            for b in range(NO):
                o = b * B + rng.permutation(np.flatnonzero(can[r, g, b * B:(b + 1) * B])); n = int(rng.choice(np.array([0, 1, K - 1, K, K + 1, B])))
                if r == 0 and b == 0: n = (K, K + 1, B, K - 1, 1, 0, K, K + 1)[g]
                pick[r, g, o[:n]] = True
    a = np.where(c[:, :, None], np.where(pick[:, :, None], rng.integers(150, 256, a.shape), rng.integers(0, 51, a.shape)), a)
    a = np.where(z[:, :, None], rng.integers(100, 111, a.shape), a)
    return pack(a, z.astype(np.int64), u, e)
def setup_inputs_ties(rng):
    a, m, u, e = parts(rng); z = firsts(e)
    lo = np.array([0, 254, 100, 0, 7, 127, 1, 128]).reshape(1, 8, 1, 1); step = np.array([1, 1, 1, 255, 1, 1, 2, 1]).reshape(1, 8, 1, 1)
    p = np.where(z, 0.6, 0.15 + 0.3 * rng.random((N, 8, V)))[:, :, None]
    a = lo + step * (rng.random(a.shape) < p)
    a[:, 1] = np.where((rng.random((N, V)) < 0.6)[:, None], 255, a[:, 1])
    return pack(a, m, u, e)
def setup_inputs_meet(rng):
    a, m, u, e = parts(rng)
    u[:, ::2] = u[:, ::2, :1].copy(); e[:, ::2] = e[:1, ::2, :1].copy()
    i = 1 + np.argsort(rng.random((N, 4, NO, B - 2)), axis=-1)[..., :K - 2]
    e[:, 1::2, :, 2:] = i; e[:, 1::2, :, 0] = 0; e[:, 1::2, :, 1] = B - 1
    base = np.arange(16 * B).reshape(B, 16).T; u[:, 1] = base; u[:, 1, NO:] = base + V - 16 * B
    o = np.argsort((np.arange(V) + rng.integers(0, 16, (N, 1, 1))) % 16 + rng.random((N, 1, V)), axis=-1)
    u[:, 2] = aim(rng, e, 2, np.broadcast_to(o, (N, NB, V)))[:, :1]
    u[:, 3] = aim(rng, e, 3, cover(rng)); z = firsts(e)
    a[:, 3] = np.where(z[:, 3][:, None], rng.integers(0, 51, (N, 15, V)), rng.integers(150, 256, (N, 15, V))); m[:, 3] = 0
    return pack(a, m, u, e)
def setup_inputs_dry(rng):
    a, m, u, e = parts(rng); z = firsts(e); o = rng.permutation(8)
    a[:, o[1]] = np.where(z[:, o[1]][:, None], rng.integers(100, 256, (N, 15, V)), rng.integers(0, 100, (N, 15, V)))
    for g in (o[3], o[4]):
        a[:, g] = np.where(rng.random((N, 15, V)) < 0.7, 255, rng.integers(0, 101, (N, 15, V)))
    a[:, o[3], :, ::B] = 0
    u[:, o[5]] = aim(rng, e, o[5], cover(rng))
    a[:, o[5]] = np.where(z[:, o[5]][:, None], rng.integers(0, 31, (N, 15, V)), rng.integers(80, 256, (N, 15, V)))
    a[:, o[5], :, ::B] = rng.integers(60, 101, (N, 15, NO))
    m[:, o[0]] = 1; m[:, o[2]] = rng.random((N, V)) < 0.9; m[:, o[3]] = 1; m[:, o[4]] = rng.random((N, V)) < 0.95
    m[:, o[5]] = 1; m[:, o[5], ::B] = 0
    m[(rng.integers(-2, 1) + np.arange(3)) % N] = 1
    return pack(a, m, u, e)
def setup_inputs_spread(rng):
    a, m, u, e = parts(rng); s = np.exp2(8.2 * rng.random((N, 8, 1, V)))
    a = np.minimum((s * rng.random(a.shape)).astype(np.int64), 255); m = (rng.random(m.shape) < rng.random((N, 8, 1)) * 0.5).astype(np.int64)
    return pack(a, m, u, e)
def check_inputs(d):
    bad = []
    r = d["rec"].astype(np.float32).reshape(N, 8, 16, V); a, m = r[:, :, :15], r[:, :, 15]
    if not np.all((a >= 0) & (a <= 255) & (a == np.floor(a))): bad.append("notes in rec")
    if not np.all((m == 0) | (m == 1)): bad.append("marks in rec")
    if np.min(d["up"]) < 0 or np.max(d["up"]) > V - 1: bad.append("range of up")
    u = np.sort(d["up"].reshape(N, 8, 16, NB, B).transpose(0, 1, 3, 2, 4).reshape(N, 8, NB, 16 * B), axis=-1)
    if np.any(u[..., 1:] == u[..., :-1]): bad.append("different parents in a bank of up")
    if np.min(d["fr"]) < 0 or np.max(d["fr"]) > B - 1: bad.append("range of fr")
    e = np.sort(np.stack([gentries(z) for z in d["fr"]]).reshape(N, 8, NO, K), axis=-1)
    if np.any(e[..., 1:] == e[..., :-1]): bad.append("different places in a bank of fr")
    return bad
def reference(rec, up, fr):
    s = rec.astype(np.float32).astype(np.int64).reshape(N, 8, 16, V); a = s[:, :, :15].copy(); mark = s[:, :, 15] > 0
    u = up.astype(np.int64).reshape(N, 8, 16, NB, B)
    e = np.stack([gentries(z) for z in fr]).astype(np.int64).reshape(N, 8, NO, K); live = np.ones(e.shape, bool)
    for wave in range(RO):
        node = e + B * np.arange(NO)[:, None]
        x = np.take_along_axis(a, node.reshape(N, 8, 1, NO * K), 3).reshape(N, 8, 15, NO, K)
        ee, ll, xx = every(e), every(live), every(np.moveaxis(x, 2, 3))
        new = a.copy(); hit = np.zeros((N, 8, V), bool)
        for b in range(NB):
            q = np.take_along_axis(u[:, :, :, b], ee[:, :, None, b], 3).reshape(N, 8, 1, 16 * K)
            old = np.take_along_axis(a, q, 3)
            arr = np.tile(xx[:, :, b], (1, 1, 1, 16))
            ok = (np.add.reduce((old >= arr).astype(np.int64), axis=2) >= TH) & np.tile(ll[:, :, b], (1, 1, 16))
            r, g, j = np.nonzero(ok); to = q[r, g, 0, j]
            new[r, g, :, to] = ((old + arr) >> 1)[r, g, :, j]
            hit[r, g, to] = True
        h = (hit & ~mark).reshape(N, 8, NO, B); mark = mark | hit; a = new
        e = np.argsort(~h, axis=-1, kind="stable")[..., :K]; live = np.take_along_axis(h, e, 3)
    return {"y": np.concatenate([a, mark[:, :, None].astype(np.int64)], axis=2).reshape(N, 128, V).astype(np.float32).astype(BF)}

@@ -1,0 +1,384 @@
+import numpy as np
+from concourse.bass import DstId, RemoteDMATransfer
+from concourse.mybir import AluOpType as OP, ActivationFunctionType as AF
+
+V, NO, B, K, RO, D = 3200, 20, 160, 8, 5, 4
+SENT = V
+GH = V + 16
+UPW = GH + D * B + 16
+STEP, SHIFT = 1680, 4896
+WIN = SHIFT + 15 * STEP + 128
+MAGIC = 8388608.0
+PKW = 34
+SLOT = 48
+
+SCRATCH = {
+    "St0": ("sbuf", [128, WIN], "bfloat16"), "St1": ("sbuf", [128, WIN], "bfloat16"),
+    "UPS": ("sbuf", [128, UPW], "int32"), "FR": ("sbuf", [128, 10], "int32"),
+    "OG": ("sbuf", [128, 3072], "bfloat16"), "CM": ("sbuf", [128, 3072], "bfloat16"), "OF": ("sbuf", [128, 3072], "bfloat16"),
+    "LF": ("sbuf", [128, 48], "float32"), "LP": ("sbuf", [128, 12], "uint16"),
+    "PQ": ("sbuf", [128, 192], "uint16"), "QF": ("sbuf", [128, 192], "float32"),
+    "XF": ("sbuf", [128, 192], "float32"), "OX": ("sbuf", [128, 192], "uint16"),
+    "PK": ("sbuf", [128, RO * SLOT], "bfloat16"), "LAND": ("sbuf", [128, RO * D * SLOT], "bfloat16"),
+    "XG": ("sbuf", [128, 128], "bfloat16"), "GX": ("sbuf", [128, 32], "bfloat16"),
+    "XT0": ("sbuf", [128, 128], "bfloat16"), "XT1": ("sbuf", [128, 128], "bfloat16"),
+    "XT2": ("sbuf", [128, 128], "bfloat16"), "XT3": ("sbuf", [128, 128], "bfloat16"),
+    "MB": ("sbuf", [128, 1600], "bfloat16"), "CC": ("sbuf", [128, 1600], "bfloat16"),
+    "IN": ("sbuf", [128, 1600], "bfloat16"), "PC": ("sbuf", [128, 1600], "bfloat16"), "RST": ("sbuf", [128, 1600], "bfloat16"),
+    "ONE": ("sbuf", [128, 1536], "bfloat16"), "E0": ("sbuf", [128, 1536], "bfloat16"),
+    "ED": ("sbuf", [128, 1536], "bfloat16"), "ES": ("sbuf", [128, 1536], "bfloat16"),
+    "ID": ("sbuf", [128, 128], "bfloat16"), "IZ": ("sbuf", [128, 128], "bfloat16"), "HB": ("sbuf", [128, 128], "bfloat16"),
+    "Z": ("sbuf", [128, 144], "bfloat16"), "T8": ("sbuf", [128, 16], "bfloat16"), "TR": ("sbuf", [128, 32], "bfloat16"),
+    "TI": ("sbuf", [128, 32], "float32"),
+    "S0": ("sbuf", [128, 128], "bfloat16"), "S1": ("sbuf", [128, 128], "bfloat16"), "MAG": ("sbuf", [128, 128], "bfloat16"),
+    "KI": ("sbuf", [128, 8], "int32"), "CF": ("sbuf", [128, 64], "float32"), "CB": ("sbuf", [128, 2], "bfloat16"),
+}
+for _i in range(8):
+    SCRATCH["P%d" % _i] = ("psum", [128, 512], "float32")
+SEMAPHORES = ["sP", "sA", "sD", "sG", "dfr", "drec", "dup0", "dup1", "dup2", "dup3", "dup4", "dup5", "dy", "snt"] + ["arr%d" % w for w in range(RO)]
+
+
+def rank_program(g, core, T, topo):
+    rank = T.rank_of(core)
+    if rank is None:
+        return
+    queues = {"P": g.tensor, "A": g.scalar, "D": g.vector, "G": g, "S": g.sync}
+    count = {"P": 0, "A": 0, "D": 0, "G": 0}
+    know = {q: {} for q in queues}
+    hist = {}
+
+    def deps(q, reads, writes):
+        found = []
+        for acc, wr in ((reads, False), (writes, True)):
+            for buf, a, b in acc:
+                psum = buf[0] == "P" and buf[1:].isdigit()
+                for e in hist.get(buf, []):
+                    if psum:
+                        if e[3] != q:
+                            found.append(e)
+                    elif e[0] < b and e[1] > a:
+                        if e[2] or (wr and e[3] != q):
+                            found.append(e)
+        k = know[q]
+        best = {}
+        for e in found:
+            if k.get(e[4], 0) >= e[5] or any(f is not e and f[6].get(e[4], 0) >= e[5] for f in found):
+                continue
+            best[e[4]] = max(best.get(e[4], 0), e[5])
+        for s, v in best.items():
+            queues[q].wait_ge(T.sem[s], v)
+        for e in found:
+            k[e[4]] = max(k.get(e[4], 0), e[5])
+            for s, v in e[6].items():
+                k[s] = max(k.get(s, 0), v)
+
+    def note(q, reads, writes, sem, val, snap):
+        for acc, wr in ((reads, False), (writes, True)):
+            for buf, a, b in acc:
+                h = hist.setdefault(buf, [])
+                if wr:
+                    h[:] = [e for e in h if not (a <= e[0] and e[1] <= b)]
+                else:
+                    h[:] = [e for e in h if not (not e[2] and e[3] == q and e[4] == sem and a <= e[0] and e[1] <= b)]
+                h.append((a, b, wr, q, sem, val, snap))
+
+    def run(q, reads, writes, f):
+        deps(q, reads, writes)
+        snap = dict(know[q])
+        count[q] += 1
+        f().then_inc(T.sem["s" + q], 1)
+        note(q, reads, writes, "s" + q, count[q], snap)
+
+    def dma(q, sem, reads, writes, out, in_):
+        deps(q, reads, writes)
+        snap = dict(know[q])
+        queues[q].dma_start(out, in_).then_inc(T.sem[sem], 16)
+        note("dma" + sem, reads, writes, sem, 16, snap)
+
+    vec, act, ten = g.vector, g.scalar, g.tensor
+
+    def ap(x, n=128, p0=0):
+        s = x[3] if len(x) > 3 else 1
+        return T[x[0]][p0:p0 + n, x[1]:x[2]:s] if s != 1 else T[x[0]][p0:p0 + n, x[1]:x[2]]
+
+    def rg(*xs):
+        return [x[:3] for x in xs]
+
+    def memset(x, c, n=128, p0=0):
+        run("D", [], rg(x), lambda: vec.memset(ap(x, n, p0), c))
+
+    def ts(out, in0, s1, s2, op0, op1=None, n=128):
+        rd = [in0] + [s for s in (s1, s2) if isinstance(s, tuple)]
+        a1 = ap(s1, n) if isinstance(s1, tuple) else s1
+        a2 = ap(s2, n) if isinstance(s2, tuple) else s2
+        if op1 is None:
+            run("D", rg(*rd), rg(out), lambda: vec.tensor_scalar(ap(out, n), ap(in0, n), a1, None, op0))
+        else:
+            run("D", rg(*rd), rg(out), lambda: vec.tensor_scalar(ap(out, n), ap(in0, n), a1, a2, op0, op1))
+
+    def tt(out, a, b, op):
+        run("D", rg(a, b), rg(out), lambda: vec.tensor_tensor(ap(out), ap(a), ap(b), op))
+
+    def cp(out, in_):
+        run("D", rg(in_), rg(out), lambda: vec.tensor_copy(ap(out), ap(in_)))
+
+    def acp(out, in_, n=128):
+        run("A", rg(in_), rg(out), lambda: act.activation(ap(out, n), ap(in_, n), AF.Copy))
+
+    def mm(out, lhsT, rhs, start, stop, m=128, k=128):
+        run("P", rg(lhsT, rhs), rg(out), lambda: ten.matmul(ap(out, m), ap(lhsT, k), ap(rhs, k), start, stop))
+
+    dma("S", "dfr", [], [("FR", 0, 10)], T.FR[:], T.fr[:])
+    dma("A", "dup0", [], [("UPS", 0, 640)], T.UPS[:, 0:640], T.up[:, 0:640])
+    dma("S", "drec", [], [("St0", 0, V)], T.St0[:, 0:V], T.rec[:])
+    for i in range(1, 5):
+        dma("SA"[i % 2], "dup%d" % i, [], [("UPS", 640 * i, 640 * i + 640)], T.UPS[:, 640 * i:640 * i + 640], T.up[:, 640 * i:640 * i + 640])
+    dma("S", "dup5", [], [("UPS", GH, GH + 640)], T.UPS[:, GH:GH + 640], T.up[:, V:V + 640])
+
+    memset(("ONE", 0, 1536), 1.0)
+
+    def iota(x, pat, base, cm, small=True):
+        if small:
+            run("G", [], rg(x), lambda: g.iota(ap(x), pat, base, cm, allow_small_or_imprecise_dtypes=True))
+        else:
+            run("G", [], rg(x), lambda: g.iota(ap(x), pat, base, cm))
+
+    def sel(out, in_, pat, op, base, cm, n=128):
+        run("G", rg(in_), rg(out), lambda: g.affine_select(ap(out, n), ap(in_, n), pat, op, 0.0, base, cm))
+
+    iota(("KI", 0, 1), [[0, 1]], 0, 1, False)
+    iota(("CF", 16, 26), [[320, 10]], 0, 0)
+    iota(("CF", 32, 34), [[320, 2]], GH, 0)
+    iota(("TI", 0, 32), [[0, 4], [16, 8]], 0, 0)
+    sel(("ID", 0, 128), ("ONE", 0, 128), [[-1, 128]], OP.is_equal, 0, 1)
+    sel(("E0", 0, 1536), ("ONE", 0, 1536), [[-1, 96], [0, 16]], OP.is_equal, 0, 1, n=96)
+    sel(("T8", 0, 8), ("ONE", 0, 8), [[-16, 8]], OP.is_ge, 0, 1)
+    sel(("T8", 8, 16), ("T8", 0, 8), [[16, 8]], OP.is_ge, 14, -1)
+    sel(("S0", 0, 128), ("ONE", 0, 128), [[-16, 8], [-1000, 2], [0, 8]], OP.is_equal, -15, 1)
+    sel(("S1", 0, 128), ("ONE", 0, 128), [[-16, 8], [-1000, 2], [0, 8]], OP.is_equal, 985, 1)
+
+    C = {n: ("CF", j, j + 1) for j, n in enumerate(["p", "m0", "p160", "r", "scol", "hbias", "lscale", "lbias", "hcol", "t"])}
+    THR, CAP = ("CB", 0, 1), ("CB", 1, 2)
+    ts(("KI", 1, 2), ("KI", 0, 1), 3, 1, OP.logical_shift_right, OP.bitwise_and)
+    ts(("KI", 2, 3), ("KI", 0, 1), 7, None, OP.bitwise_and)
+    ts(("KI", 3, 4), ("KI", 0, 1), 15, None, OP.bitwise_and)
+    cp(C["p"], ("KI", 1, 2))
+    ts(C["p160"], ("KI", 1, 2), 160.0, None, OP.mult)
+    ts(("CF", 36, 46), ("CF", 16, 26), C["p160"], None, OP.add)
+    ts(("CF", 46, 48), ("CF", 32, 34), C["p160"], None, OP.add)
+    cp(("LF", 0, 10), ("FR", 0, 10))
+    cp(C["t"], ("KI", 3, 4))
+    ts(C["r"], C["t"], 15.0, None, OP.is_equal)
+    ts(C["scol"], C["r"], -2.0, 1.0, OP.mult, OP.add)
+    ts(CAP, C["r"], -254.0, 255.0, OP.mult, OP.add)
+    ts(C["m0"], C["p"], -1.0, 1.0, OP.mult, OP.add)
+    ts(C["hbias"], C["r"], -MAGIC, None, OP.add)
+    ts(C["lscale"], C["r"], -1.0, 1.0, OP.mult, OP.add)
+    ts(C["lbias"], C["r"], MAGIC + 1.0, -MAGIC, OP.mult, OP.add)
+    ts(C["hcol"], C["r"], 254.5, 0.5, OP.mult, OP.add)
+    ts(THR, ("KI", 2, 3), 256.0, 256.0, OP.mult, OP.add)
+    for x in ("XT0", "XT1", "XT2", "XT3"):
+        memset((x, 0, 128), 0.0)
+        memset((x, 0, 128), -0.25, n=1, p0=96)
+    memset(("MAG", 0, 128), MAGIC)
+    memset(("Z", 0, 144), 0.0)
+    memset(("St0", V, V + 16), 512.0)
+    memset(("St1", V, V + 16), 512.0)
+    memset(("UPS", V, V + 16), 0)
+    memset(("UPS", GH + 640, UPW), 0)
+    ts(("IZ", 0, 128), ("ID", 0, 128), C["lscale"], None, OP.mult)
+    ts(("HB", 0, 128), ("ID", 0, 128), C["hcol"], None, OP.mult)
+
+    def late_constants():
+        ts(("ED", 0, 1536), ("E0", 0, 1536), -1.0, None, OP.mult, n=96)
+        memset(("ES", 0, 1536), 1.0, n=1, p0=96)
+        ts(("ES", 0, 1536), ("E0", 0, 1536), 0.5, None, OP.mult, n=96)
+        ts(("Z", 15, 128, 16), ("T8", 8, 16), float(-STEP), None, OP.mult)
+        ts(("TR", 0, 32), ("TI", 0, 32), C["t"], None, OP.add)
+        memset(("RST", 0, 1600), 1.0)
+        memset(("RST", 0, 1600, 160), 0.0)
+
+    dests = [T.cores[(rank + d) % 8] for d in range(1, D + 1)]
+    pick, used = {}, set()
+    for dst in sorted(dests, key=lambda c: len(topo.engines(core, c))):
+        e = [x for x in topo.engines(core, dst) if x not in used][:2]
+        used.update(e)
+        pick[dst] = sum(1 << x for x in e)
+
+    for w in range(RO):
+        X, Y = "St%d" % (w % 2), "St%d" % ((w + 1) % 2)
+        last = w == RO - 1
+        pk = SLOT * w
+
+        def gather_up(c0, c1, win):
+            a, b = 16 * c0, 16 * c1
+            run("D", [("LP", c0, c1), ("UPS", 0, win)], [("PQ", a, b)],
+                lambda: vec.tensor_copy(T.PQ[:, a:b], T.UPS[:, 0:win].indirect(T.LP[:, c0:c1])))
+            ts(("QF", a, b), ("PQ", a, b), float(-SHIFT), None, OP.add)
+
+        def gather_x(out, c0, c1):
+            run("A", [("LP", c0, c1), (X, 0, GH)], rg(out),
+                lambda: act.activation(ap(out), T[X][:, 0:GH].indirect(T.LP[:, c0:c1]), AF.Copy))
+
+        def gather_old(i):
+            run("A", [("PQ", 32 * i, 32 * i + 32), (X, 0, GH), C["scol"], C["r"]], [("OG", 512 * i, 512 * i + 512)],
+                lambda: act.activation(T.OG[:, 512 * i:512 * i + 512], T[X][:, 0:GH].indirect(T.PQ[:, 32 * i:32 * i + 32]), AF.Relu,
+                                       bias=ap(C["r"]), scale=ap(C["scol"])))
+
+        def xtile(i):
+            return ("XT0", "XT1", "XT1", "XT1", "XT2", "XT3")[i], 512 * (0, 0, 1, 2, 0, 0)[i]
+
+        def diff(i):
+            d, (x, e) = "P%d" % (3 + i % 2), xtile(i)
+            mm((d, 0, 512), ("ID", 0, 128), ("OG", 512 * i, 512 * i + 512), True, False)
+            mm((d, 0, 512), (x, 0, 128), ("ED", e, e + 512), False, True, k=96)
+
+        def half(i):
+            s, (x, e) = "P%d" % (5 + i % 2), xtile(i)
+            mm((s, 0, 512), (x, 0, 128), ("ES", e, e + 512), True, False, k=97)
+            mm((s, 0, 512), ("HB", 0, 128), ("OG", 512 * i, 512 * i + 512), False, False)
+            mm((s, 0, 512), ("MAG", 0, 128), ("ONE", 0, 512), False, True, k=1)
+
+        def signs(i):
+            d = "P%d" % (3 + i % 2)
+            run("A", [(d, 0, 512)], [("CM", 512 * i, 512 * i + 512)],
+                lambda: act.activation(T.CM[:, 512 * i:512 * i + 512], T[d][:, 0:512], AF.Sign, bias=0.5))
+
+        def offers(i):
+            s = "P%d" % (5 + i % 2)
+            bias, scale = (C["lbias"], C["lscale"]) if last else (C["hbias"], None)
+            if scale is None:
+                run("A", [(s, 0, 512), bias], [("OF", 512 * i, 512 * i + 512)],
+                    lambda: act.activation(T.OF[:, 512 * i:512 * i + 512], T[s][:, 0:512], AF.Identity, bias=ap(bias)))
+            else:
+                run("A", [(s, 0, 512), bias, scale], [("OF", 512 * i, 512 * i + 512)],
+                    lambda: act.activation(T.OF[:, 512 * i:512 * i + 512], T[s][:, 0:512], AF.Identity, bias=ap(bias), scale=ap(scale)))
+
+        def counts(i):
+            c = "P%d" % (1 + i % 2)
+            mm((c, 0, 32), ("ID", 0, 128), ("TR", 0, 32), True, False)
+            for t in range(16):
+                mm((c, 0, 32), ("Z", 15 - t, 143 - t), ("CM", 512 * i + t, 512 * i + 512, 16), False, t == 15)
+
+        def scatter(i):
+            a, b = 32 * i, 32 * i + 32
+            tt(("XF", a, b), ("P%d" % (1 + i % 2), 0, 32), ("QF", a, b), OP.max)
+            ts(("OX", a, b), ("XF", a, b), float(SHIFT), None, OP.add)
+            for c in range(4 * i, 4 * i + 4):
+                run("D", [("OX", 8 * c, 8 * c + 8), ("OF", 128 * c, 128 * c + 128)], [(Y, 0, WIN)],
+                    lambda: vec.tensor_copy(T[Y][:, 0:WIN].indirect(T.OX[:, 8 * c:8 * c + 8]), T.OF[:, 128 * c:128 * c + 128]))
+
+        def marks(bank, pairs):
+            for n, c in enumerate(pairs):
+                for p in (0, 1):
+                    b = 2 * c + p
+                    mm((bank, 160 * n, 160 * n + 160), ("S%d" % p, 0, 128), (X, 160 * b, 160 * b + 160), p == 0, p == 1)
+
+        def places(a, b):
+            run("D", [("RST", a, b), ("MB", a, b)], [("CC", a, b)],
+                lambda: vec.tensor_tensor_scan(T.CC[:, a:b], T.RST[:, a:b], T.MB[:, a:b], 0.0, OP.mult, OP.add))
+            ts(("IN", a, b), ("CC", a, b), THR, None, OP.is_lt)
+            run("D", [("RST", a, b), ("IN", a, b)], [("PC", a, b)],
+                lambda: vec.tensor_tensor_scan(T.PC[:, a:b], T.RST[:, a:b], T.IN[:, a:b], 0.0, OP.mult, OP.add))
+
+        def fresh_copy():
+            ts((Y, 0, V), (X, 0, V), CAP, None, OP.min)
+
+        def xt(bank, col, src, n):
+            mm((bank, col, col + 128), src, ("IZ", 0, 128), True, True, m=n)
+
+        def xtcopy(out, bank, col, n):
+            acp((out, 0, 128), (bank, col, col + 128), n=n)
+
+        def send():
+            deps("G", [("PK", pk, pk + PKW)], [])
+            g.remote_dma_fused([RemoteDMATransfer(
+                dst_ids=[DstId(rid=topo.addr(dst)[0], pnc=topo.addr(dst)[1])], dma_engine_mask=pick[dst], remote_sem=T.sem["arr%d" % w],
+                src=T.PK[:, pk:pk + PKW], dst=T.LAND[:, SLOT * (D * w + d):SLOT * (D * w + d) + PKW]) for d, dst in enumerate(dests)],
+                local_sem=T.sem.snt)
+            note("R", [], [("LAND", SLOT * D * w, SLOT * D * (w + 1))], "arr%d" % w, 2 * D, {})
+            for d in range(D):
+                s = SLOT * (D * w + d) + 8 * d
+                sel(("GX", 8 * d, 8 * d + 8), ("LAND", s, s + 8), [[0, 8]], OP.is_ge, 1, 0)
+
+        def ghosts():
+            for c in range(2):
+                s1, s2 = SLOT * (D * w + 2 * c) + 32 + c, SLOT * (D * w + 2 * c + 1) + 32 + c
+                ts(("LF", 24 + c, 25 + c), ("LAND", s1, s1 + 1), C["m0"], ("CF", 46 + c, 47 + c), OP.mult, OP.add)
+                ts(("LP", 10 + c, 11 + c), ("LAND", s2, s2 + 1), C["p"], ("LF", 24 + c, 25 + c), OP.mult, OP.add)
+            gather_up(10, 12, UPW)
+
+        if w == 0:
+            tt(("LF", 12, 22), ("LF", 0, 10), ("CF", 36, 46), OP.add)
+            cp(("LP", 0, 10), ("LF", 12, 22))
+            acp(("PK", pk + 32, pk + 34), ("LF", 0, 2))
+            gather_up(0, 2, 640)
+            late_constants()
+        else:
+            marks("P0", range(0, 2))
+            acp(("MB", 0, 320), ("P0", 0, 320))
+            for bank, c0, c1 in (("P4", 2, 5), ("P6", 5, 8), ("P7", 8, 10)):
+                marks(bank, range(c0, c1))
+                acp(("MB", 160 * c0, 160 * c1), (bank, 0, 160 * (c1 - c0)))
+            places(0, 320)
+            acp(("PK", pk + 32, pk + 34), ("PC", 159, 320, 160))
+            ts(("LF", 0, 2), ("PC", 159, 320, 160), 160.0, float(SENT), OP.is_ge, OP.mult)
+            for c in range(2):
+                ts(("LP", c, c + 1), ("PC", 160 * c + 159, 160 * c + 160), ("CF", 36 + c, 37 + c), ("LF", c, c + 1), OP.add, OP.max)
+            gather_up(0, 2, UPW)
+
+        gather_x(("PK", pk, pk + 32), 0, 2)
+        gather_old(0)
+        xt("P0", 0, ("PK", pk, pk + 32), 32)
+        xtcopy("XT0", "P0", 0, 32)
+        send()
+        diff(0)
+        half(0)
+        signs(0)
+        counts(0)
+        offers(0)
+
+        if w > 0:
+            places(320, 1600)
+            tt(("LF", 12, 20), ("PC", 479, 1600, 160), ("CF", 38, 46), OP.add)
+            ts(("LF", 2, 10), ("PC", 479, 1600, 160), 160.0, float(SENT), OP.is_ge, OP.mult)
+            tt(("LF", 26, 34), ("LF", 12, 20), ("LF", 2, 10), OP.max)
+            cp(("LP", 2, 10), ("LF", 26, 34))
+            gather_up(2, 10, UPW)
+            fresh_copy()
+        else:
+            fresh_copy()
+            gather_up(2, 4, 1280)
+        gather_x(("XG", 0, 128), 2, 10)
+        xt("P7", 0, ("XG", 0, 96), 96)
+        xt("P7", 128, ("XG", 96, 128), 32)
+        xtcopy("XT1", "P7", 0, 96)
+        xtcopy("XT2", "P7", 128, 32)
+        scatter(0)
+        gather_old(1)
+        diff(1)
+        half(1)
+        for i in range(1, 6):
+            if i < 5:
+                if w == 0 and i < 4:
+                    gather_up(2 * i + 2, 2 * i + 4, 640 * i + 1280)
+                if i == 4:
+                    xt("P7", 256, ("GX", 0, 32), 32)
+                    xtcopy("XT3", "P7", 256, 32)
+                gather_old(i + 1)
+                diff(i + 1)
+            signs(i)
+            counts(i)
+            offers(i)
+            if i < 5:
+                half(i + 1)
+            scatter(i)
+            if i == 2:
+                ghosts()
+
+    dma("S", "dy", [("St%d" % (RO % 2), 0, V)], [], T.y[:], T["St%d" % (RO % 2)][:, 0:V])
+    for q in "PADG":
+        g.wait_ge(T.sem["s" + q], count[q])
+    for s in ("dfr", "drec", "dup0", "dup1", "dup2", "dup3", "dup4", "dup5", "dy"):
+        g.wait_ge(T.sem[s], 16)
+    g.wait_ge(T.sem.snt, 2 * D * RO)

@@ -2,40 +2,49 @@ import numpy as np
 from concourse.bass import DstId, RemoteDMATransfer
 from concourse.mybir import AluOpType as OP, ActivationFunctionType as AF
 
+CFG = dict(waw=True, tr=False, cv=800, cs=800, cg=560, mb=1, gh=4, vof=(), early=())
 V, NO, B, K, RO, D = 3200, 20, 160, 8, 5, 4
-SENT = V
+SW = V + 256
+DUMP = 4096
+STEP, SHIFT = 1792, 5248
+WIN = SHIFT + 15 * STEP + 128 if CFG["tr"] else DUMP + SW
 GH = V + 16
 UPW = GH + D * B + 16
-STEP, SHIFT = 1680, 4896
-WIN = SHIFT + 15 * STEP + 128
-MAGIC = 8388608.0
-PKW = 34
-SLOT = 48
+WHOLE = 1.5 * 2.0 ** 23
+COARSE = 1.5 * 2.0 ** 35
+BIG = 8192.0
+PW = B + 1
+PKW, SLOT = 34, 48
+
+
+def tag(w):
+    return 2.0 ** (9 * (w + 1))
+
 
 SCRATCH = {
     "St0": ("sbuf", [128, WIN], "bfloat16"), "St1": ("sbuf", [128, WIN], "bfloat16"),
     "UPS": ("sbuf", [128, UPW], "int32"), "FR": ("sbuf", [128, 10], "int32"),
     "OG": ("sbuf", [128, 3072], "bfloat16"), "CM": ("sbuf", [128, 3072], "bfloat16"), "OF": ("sbuf", [128, 3072], "bfloat16"),
-    "LF": ("sbuf", [128, 48], "float32"), "LP": ("sbuf", [128, 12], "uint16"),
-    "PQ": ("sbuf", [128, 192], "uint16"), "QF": ("sbuf", [128, 192], "float32"),
-    "XF": ("sbuf", [128, 192], "float32"), "OX": ("sbuf", [128, 192], "uint16"),
+    "LF": ("sbuf", [128, 16], "float32"), "LP": ("sbuf", [128, 16], "uint16"),
+    "PQ": ("sbuf", [128, 192], "uint16"), "QF": ("sbuf", [128, 192], "float32"), "OX": ("sbuf", [128, 192], "uint16"),
     "PK": ("sbuf", [128, RO * SLOT], "bfloat16"), "LAND": ("sbuf", [128, RO * D * SLOT], "bfloat16"),
-    "XG": ("sbuf", [128, 128], "bfloat16"), "GX": ("sbuf", [128, 32], "bfloat16"),
+    "XG": ("sbuf", [128, 160], "bfloat16"),
     "XT0": ("sbuf", [128, 128], "bfloat16"), "XT1": ("sbuf", [128, 128], "bfloat16"),
     "XT2": ("sbuf", [128, 128], "bfloat16"), "XT3": ("sbuf", [128, 128], "bfloat16"),
-    "MB": ("sbuf", [128, 1600], "bfloat16"), "CC": ("sbuf", [128, 1600], "bfloat16"),
-    "IN": ("sbuf", [128, 1600], "bfloat16"), "PC": ("sbuf", [128, 1600], "bfloat16"), "RST": ("sbuf", [128, 1600], "bfloat16"),
-    "ONE": ("sbuf", [128, 1536], "bfloat16"), "E0": ("sbuf", [128, 1536], "bfloat16"),
-    "ED": ("sbuf", [128, 1536], "bfloat16"), "ES": ("sbuf", [128, 1536], "bfloat16"),
-    "ID": ("sbuf", [128, 128], "bfloat16"), "IZ": ("sbuf", [128, 128], "bfloat16"), "HB": ("sbuf", [128, 128], "bfloat16"),
-    "Z": ("sbuf", [128, 144], "bfloat16"), "T8": ("sbuf", [128, 16], "bfloat16"), "TR": ("sbuf", [128, 32], "bfloat16"),
-    "TI": ("sbuf", [128, 32], "float32"),
-    "S0": ("sbuf", [128, 128], "bfloat16"), "S1": ("sbuf", [128, 128], "bfloat16"), "MAG": ("sbuf", [128, 128], "bfloat16"),
-    "KI": ("sbuf", [128, 8], "int32"), "CF": ("sbuf", [128, 64], "float32"), "CB": ("sbuf", [128, 2], "bfloat16"),
+    "MB": ("sbuf", [128, 10 * PW], "bfloat16"), "CC": ("sbuf", [128, 10 * PW], "bfloat16"), "PC": ("sbuf", [128, 10 * PW], "bfloat16"),
+    "FL": ("sbuf", [128, 6 * PW], "bfloat16"), "RS": ("sbuf", [128, 6 * PW], "bfloat16"),
+    "EI": ("sbuf", [128, 1536], "bfloat16"), "ES": ("sbuf", [128, 1536], "bfloat16"), "HB": ("sbuf", [128, 256], "bfloat16"),
+    "TI": ("sbuf", [128, 32], "float32"), "TR": ("sbuf", [128, 32], "bfloat16"), "XF": ("sbuf", [128, 192], "float32"),
+    "II": ("sbuf", [128, 128], "bfloat16"), "ID": ("sbuf", [128, 128], "bfloat16"), "IDF": ("sbuf", [128, 128], "float32"),
+    "IZ": ("sbuf", [128, 128], "bfloat16"), "DP": ("sbuf", [128, 256], "bfloat16"),
+    "Z": ("sbuf", [128, 144], "bfloat16"), "T8": ("sbuf", [128, 16], "bfloat16"), "ONE": ("sbuf", [128, 512], "bfloat16"),
+    "SI": ("sbuf", [128, 256], "float32"), "SEL": ("sbuf", [128, 256 * (RO - 1)], "bfloat16"), "MAG": ("sbuf", [128, 384], "bfloat16"),
+    "KI": ("sbuf", [128, 8], "int32"), "CF": ("sbuf", [128, 64], "float32"), "CB": ("sbuf", [128, 4], "bfloat16"),
 }
 for _i in range(8):
     SCRATCH["P%d" % _i] = ("psum", [128, 512], "float32")
-SEMAPHORES = ["sP", "sA", "sD", "sG", "dfr", "drec", "dup0", "dup1", "dup2", "dup3", "dup4", "dup5", "dy", "snt"] + ["arr%d" % w for w in range(RO)]
+SEMAPHORES = (["sP", "sA", "sD", "sG", "dfr", "drec", "dy", "snt"] + ["dup%d" % i for i in range(6)]
+              + ["arr%d" % w for w in range(RO)] + ["dcp%d" % w for w in range(RO)])
 
 
 def rank_program(g, core, T, topo):
@@ -46,6 +55,7 @@ def rank_program(g, core, T, topo):
     count = {"P": 0, "A": 0, "D": 0, "G": 0}
     know = {q: {} for q in queues}
     hist = {}
+    dmas = []
 
     def deps(q, reads, writes):
         found = []
@@ -57,7 +67,7 @@ def rank_program(g, core, T, topo):
                         if e[3] != q:
                             found.append(e)
                     elif e[0] < b and e[1] > a:
-                        if e[2] or (wr and e[3] != q):
+                        if (e[2] and (CFG["waw"] or not wr or e[3] != q)) or (wr and e[3] != q):
                             found.append(e)
         k = know[q]
         best = {}
@@ -94,6 +104,7 @@ def rank_program(g, core, T, topo):
         snap = dict(know[q])
         queues[q].dma_start(out, in_).then_inc(T.sem[sem], 16)
         note("dma" + sem, reads, writes, sem, 16, snap)
+        dmas.append(sem)
 
     vec, act, ten = g.vector, g.scalar, g.tensor
 
@@ -102,101 +113,134 @@ def rank_program(g, core, T, topo):
         return T[x[0]][p0:p0 + n, x[1]:x[2]:s] if s != 1 else T[x[0]][p0:p0 + n, x[1]:x[2]]
 
     def rg(*xs):
-        return [x[:3] for x in xs]
+        return [x[:3] for x in xs if isinstance(x, tuple)]
+
+    def val(x, n=128):
+        return ap(x, n) if isinstance(x, tuple) else x
 
     def memset(x, c, n=128, p0=0):
         run("D", [], rg(x), lambda: vec.memset(ap(x, n, p0), c))
 
     def ts(out, in0, s1, s2, op0, op1=None, n=128):
-        rd = [in0] + [s for s in (s1, s2) if isinstance(s, tuple)]
-        a1 = ap(s1, n) if isinstance(s1, tuple) else s1
-        a2 = ap(s2, n) if isinstance(s2, tuple) else s2
         if op1 is None:
-            run("D", rg(*rd), rg(out), lambda: vec.tensor_scalar(ap(out, n), ap(in0, n), a1, None, op0))
+            run("D", rg(in0, s1), rg(out), lambda: vec.tensor_scalar(ap(out, n), ap(in0, n), val(s1, n), None, op0))
         else:
-            run("D", rg(*rd), rg(out), lambda: vec.tensor_scalar(ap(out, n), ap(in0, n), a1, a2, op0, op1))
+            run("D", rg(in0, s1, s2), rg(out), lambda: vec.tensor_scalar(ap(out, n), ap(in0, n), val(s1, n), val(s2, n), op0, op1))
 
     def tt(out, a, b, op):
         run("D", rg(a, b), rg(out), lambda: vec.tensor_tensor(ap(out), ap(a), ap(b), op))
 
-    def cp(out, in_):
-        run("D", rg(in_), rg(out), lambda: vec.tensor_copy(ap(out), ap(in_)))
+    def cp(out, in_, n=128):
+        run("D", rg(in_), rg(out), lambda: vec.tensor_copy(ap(out, n), ap(in_, n)))
 
-    def acp(out, in_, n=128):
-        run("A", rg(in_), rg(out), lambda: act.activation(ap(out, n), ap(in_, n), AF.Copy))
+    def scan(out, d0, d1, first, op0, op1):
+        run("D", rg(d0, d1, first), rg(out), lambda: vec.tensor_tensor_scan(ap(out), ap(d0), ap(d1), val(first), op0, op1))
+
+    def actv(out, in_, f, bias=0.0, scale=1.0, n=128):
+        run("A", rg(in_, bias, scale), rg(out), lambda: act.activation(ap(out, n), ap(in_, n), f, bias=val(bias), scale=val(scale)))
 
     def mm(out, lhsT, rhs, start, stop, m=128, k=128):
         run("P", rg(lhsT, rhs), rg(out), lambda: ten.matmul(ap(out, m), ap(lhsT, k), ap(rhs, k), start, stop))
 
-    dma("S", "dfr", [], [("FR", 0, 10)], T.FR[:], T.fr[:])
-    dma("A", "dup0", [], [("UPS", 0, 640)], T.UPS[:, 0:640], T.up[:, 0:640])
+    def iota(x, pat, base, cm, n=128):
+        if SCRATCH[x[0]][2] == "int32":
+            run("G", [], rg(x), lambda: g.iota(ap(x, n), pat, base, cm))
+        else:
+            run("G", [], rg(x), lambda: g.iota(ap(x, n), pat, base, cm, allow_small_or_imprecise_dtypes=True))
+
+    def sel(out, in_, pat, op, base, cm):
+        run("G", rg(in_), rg(out), lambda: g.affine_select(ap(out), ap(in_), pat, op, 0.0, base, cm))
+
+    def gcopy(out, in_, n):
+        sel(out, in_, [[0, n]], OP.is_ge, 1, 0)
+
+    dma("A", "dfr", [], [("FR", 0, 10)], T.FR[:], T.fr[:])
     dma("S", "drec", [], [("St0", 0, V)], T.St0[:, 0:V], T.rec[:])
+    dma("A", "dup0", [], [("UPS", 0, 640)], T.UPS[:, 0:640], T.up[:, 0:640])
     for i in range(1, 5):
-        dma("SA"[i % 2], "dup%d" % i, [], [("UPS", 640 * i, 640 * i + 640)], T.UPS[:, 640 * i:640 * i + 640], T.up[:, 640 * i:640 * i + 640])
+        dma("S", "dup%d" % i, [], [("UPS", 640 * i, 640 * i + 640)], T.UPS[:, 640 * i:640 * i + 640], T.up[:, 640 * i:640 * i + 640])
     dma("S", "dup5", [], [("UPS", GH, GH + 640)], T.UPS[:, GH:GH + 640], T.up[:, V:V + 640])
 
-    memset(("ONE", 0, 1536), 1.0)
-
-    def iota(x, pat, base, cm, small=True):
-        if small:
-            run("G", [], rg(x), lambda: g.iota(ap(x), pat, base, cm, allow_small_or_imprecise_dtypes=True))
-        else:
-            run("G", [], rg(x), lambda: g.iota(ap(x), pat, base, cm))
-
-    def sel(out, in_, pat, op, base, cm, n=128):
-        run("G", rg(in_), rg(out), lambda: g.affine_select(ap(out, n), ap(in_, n), pat, op, 0.0, base, cm))
-
-    iota(("KI", 0, 1), [[0, 1]], 0, 1, False)
-    iota(("CF", 16, 26), [[320, 10]], 0, 0)
-    iota(("CF", 32, 34), [[320, 2]], GH, 0)
+    C = {n: ("CF", j, j + 1) for j, n in enumerate(["p", "m0", "p160", "r", "scol", "obias", "nr", "t", "zc", "own", "ghost", "thr"])}
+    SC = [("CF", 12 + w, 13 + w) for w in range(RO)]
+    BASE = ("CF", 36, 46)
+    CAP, GB = ("CB", 0, 1), ("CB", 2, 4)
+    iota(("KI", 0, 1), [[0, 1]], 0, 1)
+    iota(("CF", 20, 30), [[320, 10]], 0, 0)
+    iota(("II", 0, 128), [[-1, 128]], 0, 1)
+    iota(("EI", 0, 512), [[-1, 32], [0, 16]], 0, 1, n=96)
+    memset(("ONE", 0, 512), 1.0)
+    memset(("MAG", 256, 384), WHOLE, n=1)
     iota(("TI", 0, 32), [[0, 4], [16, 8]], 0, 0)
-    sel(("ID", 0, 128), ("ONE", 0, 128), [[-1, 128]], OP.is_equal, 0, 1)
-    sel(("E0", 0, 1536), ("ONE", 0, 1536), [[-1, 96], [0, 16]], OP.is_equal, 0, 1, n=96)
     sel(("T8", 0, 8), ("ONE", 0, 8), [[-16, 8]], OP.is_ge, 0, 1)
-    sel(("T8", 8, 16), ("T8", 0, 8), [[16, 8]], OP.is_ge, 14, -1)
-    sel(("S0", 0, 128), ("ONE", 0, 128), [[-16, 8], [-1000, 2], [0, 8]], OP.is_equal, -15, 1)
-    sel(("S1", 0, 128), ("ONE", 0, 128), [[-16, 8], [-1000, 2], [0, 8]], OP.is_equal, 985, 1)
-
-    C = {n: ("CF", j, j + 1) for j, n in enumerate(["p", "m0", "p160", "r", "scol", "hbias", "lscale", "lbias", "hcol", "t"])}
-    THR, CAP = ("CB", 0, 1), ("CB", 1, 2)
+    sel(("T8", 8, 16), ("T8", 0, 8), [[16, 8]], OP.is_ge, 15, -1)
+    iota(("EI", 512, 1536), [[-1, 64], [0, 16]], -32, 1, n=96)
+    memset(("St0", V, SW), 0.0)
+    memset(("St1", V, SW), 0.0)
+    memset(("MAG", 0, 128), COARSE, n=1)
+    memset(("MAG", 128, 256), -COARSE, n=1)
+    memset(("Z", 0, 144), 0.0)
+    for x in ("XT0", "XT1", "XT2", "XT3"):
+        memset((x, 0, 128), 0.0, n=96)
+        memset((x, 0, 128), 1.0, n=1, p0=96)
     ts(("KI", 1, 2), ("KI", 0, 1), 3, 1, OP.logical_shift_right, OP.bitwise_and)
     ts(("KI", 2, 3), ("KI", 0, 1), 7, None, OP.bitwise_and)
     ts(("KI", 3, 4), ("KI", 0, 1), 15, None, OP.bitwise_and)
-    cp(C["p"], ("KI", 1, 2))
+    for x in ("XT0", "XT1", "XT2", "XT3"):
+        run("D", [(x, 0, 128)], [(x, 0, 128)], lambda: vec.memset(T[x][96:97, 15:128:16], 0.0))
     ts(C["p160"], ("KI", 1, 2), 160.0, None, OP.mult)
-    ts(("CF", 36, 46), ("CF", 16, 26), C["p160"], None, OP.add)
-    ts(("CF", 46, 48), ("CF", 32, 34), C["p160"], None, OP.add)
-    cp(("LF", 0, 10), ("FR", 0, 10))
-    cp(C["t"], ("KI", 3, 4))
-    ts(C["r"], C["t"], 15.0, None, OP.is_equal)
+    ts(C["r"], ("KI", 3, 4), 15.0, None, OP.is_equal)
+    cp(C["p"], ("KI", 1, 2))
+    ts(C["own"], ("KI", 2, 3), float(V), None, OP.add)
+    ts(C["ghost"], ("KI", 2, 3), float(D * B), None, OP.add)
+    ts(C["thr"], ("KI", 2, 3), BIG, BIG, OP.mult, OP.add)
+    ts(BASE, ("CF", 20, 30), C["p160"], None, OP.add)
     ts(C["scol"], C["r"], -2.0, 1.0, OP.mult, OP.add)
+    ts(C["nr"], C["r"], -1.0, 1.0, OP.mult, OP.add)
     ts(CAP, C["r"], -254.0, 255.0, OP.mult, OP.add)
     ts(C["m0"], C["p"], -1.0, 1.0, OP.mult, OP.add)
-    ts(C["hbias"], C["r"], -MAGIC, None, OP.add)
-    ts(C["lscale"], C["r"], -1.0, 1.0, OP.mult, OP.add)
-    ts(C["lbias"], C["r"], MAGIC + 1.0, -MAGIC, OP.mult, OP.add)
-    ts(C["hcol"], C["r"], 254.5, 0.5, OP.mult, OP.add)
-    ts(THR, ("KI", 2, 3), 256.0, 256.0, OP.mult, OP.add)
-    for x in ("XT0", "XT1", "XT2", "XT3"):
-        memset((x, 0, 128), 0.0)
-        memset((x, 0, 128), -0.25, n=1, p0=96)
-    memset(("MAG", 0, 128), MAGIC)
-    memset(("Z", 0, 144), 0.0)
-    memset(("St0", V, V + 16), 512.0)
-    memset(("St1", V, V + 16), 512.0)
-    memset(("UPS", V, V + 16), 0)
-    memset(("UPS", GH + 640, UPW), 0)
-    ts(("IZ", 0, 128), ("ID", 0, 128), C["lscale"], None, OP.mult)
-    ts(("HB", 0, 128), ("ID", 0, 128), C["hcol"], None, OP.mult)
+    if CFG["tr"]:
+        ts(C["zc"], C["r"], float(SHIFT + STEP), -float(STEP), OP.mult, OP.add)
+    else:
+        ts(C["zc"], C["r"], 2304.0 + 128.0, -128.0, OP.mult, OP.add)
+    ts(C["obias"], C["r"], WHOLE + 1, -WHOLE, OP.mult, OP.add)
+    cp(C["t"], ("KI", 3, 4))
+    memset(("MAG", 256 + 15, 384, 16), 0.0, n=1)
+    cp(GB, ("CF", 36, 38))
+    ts(("ID", 0, 128), ("II", 0, 128), 0.0, None, OP.is_equal)
+    ts(("HB", 0, 128), ("II", 0, 128), 0.0, 0.5, OP.is_equal, OP.mult)
+    ts(("HB", 128, 256), ("II", 0, 128), 0.0, -0.5, OP.is_equal, OP.mult)
+    ts(("TR", 0, 32), ("TI", 0, 32), C["t"], None, OP.add)
+    for w in range(RO):
+        ts(SC[w], C["r"], 2 * tag(w) if w < RO - 1 else 0.0, C["nr"], OP.mult, OP.add)
+    ts(("IZ", 0, 128), ("II", 0, 128), 0.0, C["nr"], OP.is_equal, OP.mult)
+    ts(("IDF", 0, 128), ("II", 0, 128), 0.0, None, OP.is_equal)
+    run("D", [("T8", 8, 16), C["zc"], ("Z", 0, 144)], [("Z", 0, 144)],
+        lambda: vec.tensor_scalar(T.Z[:, 15:128:16], T.T8[:, 8:16], ap(C["zc"]), None, OP.mult))
 
-    def late_constants():
-        ts(("ED", 0, 1536), ("E0", 0, 1536), -1.0, None, OP.mult, n=96)
-        memset(("ES", 0, 1536), 1.0, n=1, p0=96)
-        ts(("ES", 0, 1536), ("E0", 0, 1536), 0.5, None, OP.mult, n=96)
-        ts(("Z", 15, 128, 16), ("T8", 8, 16), float(-STEP), None, OP.mult)
-        ts(("TR", 0, 32), ("TI", 0, 32), C["t"], None, OP.add)
-        memset(("RST", 0, 1600), 1.0)
-        memset(("RST", 0, 1600, 160), 0.0)
+    def spreads(a, b):
+        memset(("ES", a, b), -0.25, n=1, p0=96)
+        ts(("ES", a, b), ("EI", a, b), 0.0, 0.5, OP.is_equal, OP.mult, n=96)
+
+    spreads(0, 512)
+
+    def late_gpsimd():
+        iota(("UPS", V, V + 16), [[16, 16]], V, 1)
+        iota(("UPS", GH + D * B, UPW), [[16, 16]], V, 1)
+        iota(("SI", 0, 128), [[-16, 8], [-1000, 2], [0, 8]], -15, 1)
+        iota(("SI", 128, 256), [[-16, 8], [-1000, 2], [0, 8]], 985, 1)
+        iota(("FL", 0, 6 * PW), [[0, 6], [1, PW]], 0, 0)
+
+    def late_vector():
+        ts(("DP", 0, 128), ("II", 0, 128), 0.0, C["m0"], OP.is_equal, OP.mult)
+        ts(("DP", 128, 256), ("II", 0, 128), 0.0, C["p"], OP.is_equal, OP.mult)
+        memset(("RS", 0, 6 * PW), 0.0)
+
+    def later_vector():
+        run("D", [("RS", 0, 6 * PW)], [("RS", 0, 6 * PW)], lambda: vec.memset(T.RS[:, B:6 * PW:PW], 2.0 ** 20))
+        for w in range(RO - 1):
+            ts(("SEL", 256 * w, 256 * w + 256), ("SI", 0, 256), 0.0, -BIG / tag(w), OP.is_equal, OP.mult)
+        ts(("FL", B, 6 * PW, PW), ("ONE", 0, 6), C["thr"], None, OP.mult)
 
     dests = [T.cores[(rank + d) % 8] for d in range(1, D + 1)]
     pick, used = {}, set()
@@ -205,90 +249,120 @@ def rank_program(g, core, T, topo):
         used.update(e)
         pick[dst] = sum(1 << x for x in e)
 
+    CH = [(0, 1, "XT0", 0), (1, 2, "XT0", 16), (2, 4, "XT1", 0), (4, 6, "XT2", 0), (6, 8, "XT2", 32), (8, 10, "XT2", 64), (10, 12, "XT3", 0)]
+    NC = len(CH)
     for w in range(RO):
         X, Y = "St%d" % (w % 2), "St%d" % ((w + 1) % 2)
-        last = w == RO - 1
         pk = SLOT * w
 
-        def gather_up(c0, c1, win):
+        def gather_up(c0, c1, a0, a1):
             a, b = 16 * c0, 16 * c1
-            run("D", [("LP", c0, c1), ("UPS", 0, win)], [("PQ", a, b)],
-                lambda: vec.tensor_copy(T.PQ[:, a:b], T.UPS[:, 0:win].indirect(T.LP[:, c0:c1])))
-            ts(("QF", a, b), ("PQ", a, b), float(-SHIFT), None, OP.add)
+            run("D", [("LP", c0, c1), ("UPS", a0, a1)], [("PQ", a, b)],
+                lambda: vec.tensor_copy(T.PQ[:, a:b], T.UPS[:, a0:a1].indirect(T.LP[:, c0:c1])))
+
+        def qf(c0, c1):
+            cp(("QF", 16 * c0, 16 * c1), ("PQ", 16 * c0, 16 * c1))
 
         def gather_x(out, c0, c1):
-            run("A", [("LP", c0, c1), (X, 0, GH)], rg(out),
-                lambda: act.activation(ap(out), T[X][:, 0:GH].indirect(T.LP[:, c0:c1]), AF.Copy))
+            run("A", [("LP", c0, c1), (X, 0, SW)], rg(out),
+                lambda: act.activation(ap(out), T[X][:, 0:SW].indirect(T.LP[:, c0:c1]), AF.Copy))
+
+        def edges(buf, i, per=256):
+            return (buf, per * CH[i][0], per * CH[i][1])
 
         def gather_old(i):
-            run("A", [("PQ", 32 * i, 32 * i + 32), (X, 0, GH), C["scol"], C["r"]], [("OG", 512 * i, 512 * i + 512)],
-                lambda: act.activation(T.OG[:, 512 * i:512 * i + 512], T[X][:, 0:GH].indirect(T.PQ[:, 32 * i:32 * i + 32]), AF.Relu,
+            run("A", [edges("PQ", i, 16), (X, 0, SW), C["scol"], C["r"]], [edges("OG", i)],
+                lambda: act.activation(ap(edges("OG", i)), T[X][:, 0:SW].indirect(ap(edges("PQ", i, 16))), AF.Relu,
                                        bias=ap(C["r"]), scale=ap(C["scol"])))
 
-        def xtile(i):
-            return ("XT0", "XT1", "XT1", "XT1", "XT2", "XT3")[i], 512 * (0, 0, 1, 2, 0, 0)[i]
+        def bank(i, first):
+            return ("P%d" % (first + i % 2), 0, 256 * (CH[i][1] - CH[i][0]))
 
-        def diff(i):
-            d, (x, e) = "P%d" % (3 + i % 2), xtile(i)
-            mm((d, 0, 512), ("ID", 0, 128), ("OG", 512 * i, 512 * i + 512), True, False)
-            mm((d, 0, 512), (x, 0, 128), ("ED", e, e + 512), False, True, k=96)
+        def spread(i, first, k):
+            a = 16 * CH[i][3]
+            mm(bank(i, first), (CH[i][2], 0, 128), ("ES", a, a + bank(i, first)[2]), True, False, k=k)
 
-        def half(i):
-            s, (x, e) = "P%d" % (5 + i % 2), xtile(i)
-            mm((s, 0, 512), (x, 0, 128), ("ES", e, e + 512), True, False, k=97)
-            mm((s, 0, 512), ("HB", 0, 128), ("OG", 512 * i, 512 * i + 512), False, False)
-            mm((s, 0, 512), ("MAG", 0, 128), ("ONE", 0, 512), False, True, k=1)
+        def less(i):
+            spread(i, 3, 97)
+
+        def olds(i):
+            mm(bank(i, 3), ("HB", 128, 256), edges("OG", i), False, True)
+
+        def total(i):
+            spread(i, 5, 97)
+            mm(bank(i, 5), ("HB", 0, 128), edges("OG", i), False, False)
+            mm(bank(i, 5), ("MAG", 256, 384), ("ONE", 0, bank(i, 5)[2]), False, True, k=1)
 
         def signs(i):
-            d = "P%d" % (3 + i % 2)
-            run("A", [(d, 0, 512)], [("CM", 512 * i, 512 * i + 512)],
-                lambda: act.activation(T.CM[:, 512 * i:512 * i + 512], T[d][:, 0:512], AF.Sign, bias=0.5))
+            actv(edges("CM", i), bank(i, 3), AF.Sign, bias=0.125, scale=-1.0)
 
-        def offers(i):
-            s = "P%d" % (5 + i % 2)
-            bias, scale = (C["lbias"], C["lscale"]) if last else (C["hbias"], None)
-            if scale is None:
-                run("A", [(s, 0, 512), bias], [("OF", 512 * i, 512 * i + 512)],
-                    lambda: act.activation(T.OF[:, 512 * i:512 * i + 512], T[s][:, 0:512], AF.Identity, bias=ap(bias)))
+        def offers(i, a=0, b=None):
+            o, s = edges("OF", i), bank(i, 5)
+            b = s[2] if b is None else b
+            if i in CFG["vof"]:
+                ts(("OF", o[1] + a, o[1] + b), (s[0], a, b), SC[w], C["obias"], OP.mult, OP.add)
             else:
-                run("A", [(s, 0, 512), bias, scale], [("OF", 512 * i, 512 * i + 512)],
-                    lambda: act.activation(T.OF[:, 512 * i:512 * i + 512], T[s][:, 0:512], AF.Identity, bias=ap(bias), scale=ap(scale)))
+                actv(("OF", o[1] + a, o[1] + b), (s[0], a, b), AF.Identity, bias=C["obias"], scale=SC[w])
+
+        def cbank(i):
+            return ("P%d" % (1 + i % 2), 0, 16 * (CH[i][1] - CH[i][0]))
+
+        def count_open(i):
+            if CFG["tr"]:
+                mm(cbank(i), ("ID", 0, 128), ("TR", 0, cbank(i)[2]), True, False)
+            else:
+                mm(cbank(i), ("MAG", 0, 128), ("ONE", 0, cbank(i)[2]), True, False, k=1)
 
         def counts(i):
-            c = "P%d" % (1 + i % 2)
-            mm((c, 0, 32), ("ID", 0, 128), ("TR", 0, 32), True, False)
+            _, a, b = edges("CM", i)
             for t in range(16):
-                mm((c, 0, 32), ("Z", 15 - t, 143 - t), ("CM", 512 * i + t, 512 * i + 512, 16), False, t == 15)
+                mm(cbank(i), ("Z", 15 - t, 143 - t), ("CM", a + t, b, 16), False, CFG["tr"] and t == 15)
+            if not CFG["tr"]:
+                mm(cbank(i), ("MAG", 128, 256), ("ONE", 0, cbank(i)[2]), False, False, k=1)
+                mm(cbank(i), ("IDF", 0, 128), edges("QF", i, 16), False, True)
+
+        def targets(i):
+            if CFG["tr"]:
+                tt(edges("XF", i, 16), cbank(i), edges("QF", i, 16), OP.max)
+                cp(edges("OX", i, 16), edges("XF", i, 16))
+            else:
+                cp(edges("OX", i, 16), cbank(i))
 
         def scatter(i):
-            a, b = 32 * i, 32 * i + 32
-            tt(("XF", a, b), ("P%d" % (1 + i % 2), 0, 32), ("QF", a, b), OP.max)
-            ts(("OX", a, b), ("XF", a, b), float(SHIFT), None, OP.add)
-            for c in range(4 * i, 4 * i + 4):
+            for c in range(2 * CH[i][0], 2 * CH[i][1]):
                 run("D", [("OX", 8 * c, 8 * c + 8), ("OF", 128 * c, 128 * c + 128)], [(Y, 0, WIN)],
                     lambda: vec.tensor_copy(T[Y][:, 0:WIN].indirect(T.OX[:, 8 * c:8 * c + 8]), T.OF[:, 128 * c:128 * c + 128]))
 
-        def marks(bank, pairs):
-            for n, c in enumerate(pairs):
+        def marks(pb, c0, c1):
+            for c in range(c0, c1):
                 for p in (0, 1):
-                    b = 2 * c + p
-                    mm((bank, 160 * n, 160 * n + 160), ("S%d" % p, 0, 128), (X, 160 * b, 160 * b + 160), p == 0, p == 1)
+                    b, s = 2 * c + p, 256 * (w - 1) + 128 * p
+                    mm((pb, PW * (c - c0), PW * (c - c0 + 1)), ("SEL", s, s + 128), (X, B * b, B * b + PW), p == 0, p == 1)
 
-        def places(a, b):
-            run("D", [("RST", a, b), ("MB", a, b)], [("CC", a, b)],
-                lambda: vec.tensor_tensor_scan(T.CC[:, a:b], T.RST[:, a:b], T.MB[:, a:b], 0.0, OP.mult, OP.add))
-            ts(("IN", a, b), ("CC", a, b), THR, None, OP.is_lt)
-            run("D", [("RST", a, b), ("IN", a, b)], [("PC", a, b)],
-                lambda: vec.tensor_tensor_scan(T.PC[:, a:b], T.RST[:, a:b], T.IN[:, a:b], 0.0, OP.mult, OP.add))
+        def mcopy(pb, c0, c1):
+            actv(("MB", PW * c0, PW * c1), (pb, 0, PW * (c1 - c0)), AF.Copy)
 
-        def fresh_copy():
-            ts((Y, 0, V), (X, 0, V), CAP, None, OP.min)
+        def remaining(pb, c0, c1):
+            a, b = PW * c0, PW * c1
+            scan(("CC", a, b), (pb, 0, b - a) if pb != "MB" else (pb, a, b), ("FL", 0, b - a), C["thr"], OP.add, OP.max)
 
-        def xt(bank, col, src, n):
-            mm((bank, col, col + 128), src, ("IZ", 0, 128), True, True, m=n)
+        def places(c0, c1):
+            a, b = PW * c0, PW * c1
+            scan(("PC", a, b), ("RS", 0, b - a), ("CC", a, b), 2.0 ** 20, OP.add, OP.min)
 
-        def xtcopy(out, bank, col, n):
-            acp((out, 0, 128), (bank, col, col + 128), n=n)
+        def lists(c0, c1):
+            if c1 - c0 <= 2:
+                for c in range(c0, c1):
+                    ts(("LP", c, c + 1), ("PC", PW * c + B - 1, PW * c + B), ("CF", 36 + c, 37 + c), C["own"], OP.add, OP.min)
+            else:
+                tt(("LF", c0, c1), ("PC", PW * c0 + B - 1, PW * c1, PW), ("CF", 36 + c0, 36 + c1), OP.add)
+                ts(("LP", c0, c1), ("LF", c0, c1), C["own"], None, OP.min)
+
+        def xt(pb, col, src):
+            mm((pb, col, col + 128), src, ("IZ", 0, 128), True, True, m=src[2] - src[1])
+
+        def xtcopy(out, pb, col, n):
+            actv((out, 0, 128), (pb, col, col + 128), AF.Copy, n=n)
 
         def send():
             deps("G", [("PK", pk, pk + PKW)], [])
@@ -297,88 +371,157 @@ def rank_program(g, core, T, topo):
                 src=T.PK[:, pk:pk + PKW], dst=T.LAND[:, SLOT * (D * w + d):SLOT * (D * w + d) + PKW]) for d, dst in enumerate(dests)],
                 local_sem=T.sem.snt)
             note("R", [], [("LAND", SLOT * D * w, SLOT * D * (w + 1))], "arr%d" % w, 2 * D, {})
+
+        def ghost_notes():
             for d in range(D):
                 s = SLOT * (D * w + d) + 8 * d
-                sel(("GX", 8 * d, 8 * d + 8), ("LAND", s, s + 8), [[0, 8]], OP.is_ge, 1, 0)
+                gcopy(("XG", 128 + 8 * d, 136 + 8 * d), ("LAND", s, s + 8), 8)
 
-        def ghosts():
-            for c in range(2):
-                s1, s2 = SLOT * (D * w + 2 * c) + 32 + c, SLOT * (D * w + 2 * c + 1) + 32 + c
-                ts(("LF", 24 + c, 25 + c), ("LAND", s1, s1 + 1), C["m0"], ("CF", 46 + c, 47 + c), OP.mult, OP.add)
-                ts(("LP", 10 + c, 11 + c), ("LAND", s2, s2 + 1), C["p"], ("LF", 24 + c, 25 + c), OP.mult, OP.add)
-            gather_up(10, 12, UPW)
+        def ghost_places():
+            for p in (0, 1):
+                s = SLOT * (D * w + p) + 32
+                mm(("P0", 384, 386), ("DP", 128 * p, 128 * p + 128), ("LAND", s, s + 2 * SLOT + 2, 2 * SLOT + 1), p == 0, False)
+            mm(("P0", 384, 386), ("ID", 0, 128), GB, False, True)
+
+        def ghost_lists():
+            ts(("LP", 10, 12), ("P0", 384, 386), C["ghost"], None, OP.min)
+            gather_up(10, 12, GH, UPW)
+
+        def capped(a, b):
+            ts((Y, a, b), (X, a, b), CAP, None, OP.min)
 
         if w == 0:
-            tt(("LF", 12, 22), ("LF", 0, 10), ("CF", 36, 46), OP.add)
-            cp(("LP", 0, 10), ("LF", 12, 22))
-            acp(("PK", pk + 32, pk + 34), ("LF", 0, 2))
-            gather_up(0, 2, 640)
-            late_constants()
+            tt(("LF", 0, 10), ("FR", 0, 10), BASE, OP.add)
+            cp(("LP", 0, 10), ("LF", 0, 10))
+            cp(("PK", pk + 32, pk + 34), ("FR", 0, 2))
+            gather_up(0, 2, 0, 640)
+            qf(0, 2)
         else:
-            marks("P0", range(0, 2))
-            acp(("MB", 0, 320), ("P0", 0, 320))
-            for bank, c0, c1 in (("P4", 2, 5), ("P6", 5, 8), ("P7", 8, 10)):
-                marks(bank, range(c0, c1))
-                acp(("MB", 160 * c0, 160 * c1), (bank, 0, 160 * (c1 - c0)))
-            places(0, 320)
-            acp(("PK", pk + 32, pk + 34), ("PC", 159, 320, 160))
-            ts(("LF", 0, 2), ("PC", 159, 320, 160), 160.0, float(SENT), OP.is_ge, OP.mult)
-            for c in range(2):
-                ts(("LP", c, c + 1), ("PC", 160 * c + 159, 160 * c + 160), ("CF", 36 + c, 37 + c), ("LF", c, c + 1), OP.add, OP.max)
-            gather_up(0, 2, UPW)
+            cv, cs, cg = CFG["cv"], CFG["cs"], CFG["cg"]
+            marks("P0", 0, 2)
+            marks("P7", 2, 4)
+            marks("P5", 4, 7)
+            marks("P6", 7, 10)
+            capped(0, cv)
+            if w < RO - 1:
+                if cv + cs + cg < V:
+                    dma("S", "dcp%d" % w, [(X, cv + cs + cg, V)], [(Y, cv + cs + cg, V)], T[Y][:, cv + cs + cg:V], T[X][:, cv + cs + cg:V])
+                if cs:
+                    actv((Y, cv, cv + cs), (X, cv, cv + cs), AF.Copy)
+                if cg:
+                    gcopy((Y, cv + cs, cv + cs + cg), (X, cv + cs, cv + cs + cg), cg)
+            remaining("P0", 0, 2)
+            places(0, 2)
+            lists(0, 2)
+            if CFG["mb"]:
+                mcopy("P7", 2, 4)
+            gcopy(("PK", pk + 32, pk + 34), ("PC", B - 1, 2 * PW, PW), 2)
+            gather_up(0, 2, 0, GH)
 
         gather_x(("PK", pk, pk + 32), 0, 2)
-        gather_old(0)
-        xt("P0", 0, ("PK", pk, pk + 32), 32)
-        xtcopy("XT0", "P0", 0, 32)
+        xt("P0", 0, ("PK", pk, pk + 32))
         send()
-        diff(0)
-        half(0)
-        signs(0)
-        counts(0)
-        offers(0)
-
+        if w == 0:
+            late_gpsimd()
+        ghost_notes()
+        gather_old(0)
+        xtcopy("XT0", "P0", 0, 32)
+        count_open(0)
+        less(0)
+        olds(0)
         if w > 0:
-            places(320, 1600)
-            tt(("LF", 12, 20), ("PC", 479, 1600, 160), ("CF", 38, 46), OP.add)
-            ts(("LF", 2, 10), ("PC", 479, 1600, 160), 160.0, float(SENT), OP.is_ge, OP.mult)
-            tt(("LF", 26, 34), ("LF", 12, 20), ("LF", 2, 10), OP.max)
-            cp(("LP", 2, 10), ("LF", 26, 34))
-            gather_up(2, 10, UPW)
-            fresh_copy()
+            remaining("MB" if CFG["mb"] else "P7", 2, 4)
+            qf(0, 2)
+            places(2, 4)
+            remaining("P5", 4, 7)
+            lists(2, 4)
+            remaining("P6", 7, 10)
+            gather_up(2, 4, 0, GH)
+            places(4, 10)
+            qf(2, 4)
+            lists(4, 10)
+            if w == RO - 1:
+                capped(cv, V)
         else:
-            fresh_copy()
-            gather_up(2, 4, 1280)
-        gather_x(("XG", 0, 128), 2, 10)
-        xt("P7", 0, ("XG", 0, 96), 96)
-        xt("P7", 128, ("XG", 96, 128), 32)
-        xtcopy("XT1", "P7", 0, 96)
-        xtcopy("XT2", "P7", 128, 32)
-        scatter(0)
+            spreads(512, 1536)
+            gather_up(2, 4, 0, 1280)
+            qf(2, 4)
+            capped(0, V)
         gather_old(1)
-        diff(1)
-        half(1)
-        for i in range(1, 6):
-            if i < 5:
-                if w == 0 and i < 4:
-                    gather_up(2 * i + 2, 2 * i + 4, 640 * i + 1280)
-                if i == 4:
-                    xt("P7", 256, ("GX", 0, 32), 32)
-                    xtcopy("XT3", "P7", 256, 32)
-                gather_old(i + 1)
-                diff(i + 1)
+        less(1)
+        olds(1)
+        signs(0)
+        total(0)
+        counts(0)
+        count_open(1)
+        signs(1)
+        gather_x(("XG", 0, 32), 2, 4)
+        offers(0)
+        total(1)
+        xt("P7", 0, ("XG", 0, 32))
+        counts(1)
+        targets(0)
+        if w > 0:
+            gather_up(4, 10, 0, GH)
+        else:
+            gather_up(4, 6, 0, 1920)
+            qf(4, 6)
+        scatter(0)
+        gather_old(2)
+        xtcopy("XT1", "P7", 0, 32)
+        offers(1)
+        less(2)
+        olds(2)
+        total(2)
+        count_open(2)
+        targets(1)
+        if w > 0:
+            qf(4, 10)
+        else:
+            late_vector()
+        scatter(1)
+        gather_x(("XG", 32, 128), 4, 10)
+        xt("P7", 128, ("XG", 32, 128))
+        for i in range(2, NC):
+            if w == 0 and i < 4:
+                c = CH[i + 2][0]
+                gather_up(c, c + 2, 0, 320 * c + 640)
+                qf(c, c + 2)
             signs(i)
-            counts(i)
-            offers(i)
-            if i < 5:
-                half(i + 1)
-            scatter(i)
             if i == 2:
-                ghosts()
+                xtcopy("XT2", "P7", 128, 96)
+            counts(i)
+            if i in CFG["early"]:
+                offers(i)
+            if i + 1 < NC:
+                if i == 2:
+                    less(3)
+                gather_old(i + 1)
+                olds(i + 1)
+            if i == CFG["gh"]:
+                ghost_places()
+                xt("P0", 0, ("XG", 128, 160))
+            if i not in CFG["early"]:
+                offers(i)
+            if i == CFG["gh"]:
+                xtcopy("XT3", "P0", 0, 32)
+            if i + 1 < NC:
+                total(i + 1)
+                count_open(i + 1)
+            if i + 2 < NC:
+                less(i + 2)
+            targets(i)
+            if i == CFG["gh"]:
+                ghost_lists()
+            if i == CFG["gh"] + 1:
+                qf(10, 12)
+            if w == 0 and i == 4:
+                later_vector()
+            scatter(i)
 
     dma("S", "dy", [("St%d" % (RO % 2), 0, V)], [], T.y[:], T["St%d" % (RO % 2)][:, 0:V])
     for q in "PADG":
         g.wait_ge(T.sem["s" + q], count[q])
-    for s in ("dfr", "drec", "dup0", "dup1", "dup2", "dup3", "dup4", "dup5", "dy"):
+    for s in dmas:
         g.wait_ge(T.sem[s], 16)
     g.wait_ge(T.sem.snt, 2 * D * RO)

@@ -2,49 +2,105 @@ import numpy as np
 from concourse.bass import DstId, RemoteDMATransfer
 from concourse.mybir import AluOpType as OP, ActivationFunctionType as AF
 
-CFG = dict(waw=True, tr=False, cv=800, cs=800, cg=560, mb=1, gh=4, vof=(), early=())
+CFG = dict(cv=480, cs=800, cg=0)
 V, NO, B, K, RO, D = 3200, 20, 160, 8, 5, 4
 SW = V + 256
-DUMP = 4096
 STEP, SHIFT = 1792, 5248
-WIN = SHIFT + 15 * STEP + 128 if CFG["tr"] else DUMP + SW
+WIN = SHIFT + 15 * STEP + 128
 GH = V + 16
 UPW = GH + D * B + 16
 WHOLE = 1.5 * 2.0 ** 23
-COARSE = 1.5 * 2.0 ** 35
 BIG = 8192.0
 PW = B + 1
-PKW, SLOT = 34, 48
+XW, SLOT = 208, 48
+PIECES = ((0, 640), (640, V))
+SCANS = ((0, 1, "P0"), (1, 2, "P1"), (2, 4, "P7"), (4, 7, "P6"), (7, 10, "P2"))
+LISTS = ((0, 2), (2, 4), (4, 10))
+TILES = ((0, 2, "P0"), (2, 4, "P7"), (4, 10, "P7"), (10, 12, "P0"))
+CHUNKS = ((0, 1), (1, 2), (2, 4), (4, 6), (6, 8), (8, 10), (10, 12))
 
 
 def tag(w):
     return 2.0 ** (9 * (w + 1))
 
 
+def plan(w):
+    vector = ("cv0 rem0 rem1 pl0 pl1 li0 li1 rem2 up0 pl2 li2 li3 qf0 rem4 S0 cap rem7 up2 pl4 qf2 xf0 lf4 ox0 li4 "
+              "s0 xf1 s1 ox1 up4 s2 s3 xf2 qf4 ox2").split()
+    scalar = "cs x0 xc0 G0 G1 x2 O0 S1 xc1 G2 x4 O1 xc2 S2 G3 O2 S3 G4 O3 S4 G5 O4 S5 xc3 G6 O5 S6 O6".split()
+    tensor = ("mk0 mk1 mk2 mk3 mk4 mk5 mk6 xt0 mk7 mk8 mk9 dx1 op0 dx0 sx0 so0 sm0 sx1 do1 xt1 ct0 so1 op1 sm1 ct1 "
+              "dx2 xt2 do2 sx2 op2 so2 sm2 ct2 dx3 op3 do3 dx4 sx3 so3 sm3 ct3 do4 op4 sx4 so4 sm4 ct4 "
+              "dx5 do5 gp sx5 so5 xt3 op5 ct5 sm5 dx6 do6 sx6 op6 so6 sm6 ct6").split()
+    gpsimd = "pk send gn".split()
+    between = {6: "xf3", 7: "ox3", 9: "xf4", 10: "ox4", 11: "li10", 12: "up10", 13: "xf5", 14: "ox5", 16: "qf10", 18: "xf6", 19: "ox6"}
+    if w == 0:
+        vector = "kv0 first li0 li2 li4 kv1 up0 qf0 cv0 kv2 cv1 S0 cv2 up2 qf2 xf0 ox0 s0 up4 xf1 s1 ox1 qf4 s2 up6 s3 xf2 qf6 ox2".split()
+        scalar = ["fr", "up_0", "ks0", "ks3", "x0", "ks1", "xc0", "ks2"] + scalar[3:] + ["ks4"]
+        tensor = ["xt0", "kp"] + tensor[8:]
+        gpsimd = ["kg0", "send", "kg1", "gn"]
+        between.update({4: "up8", 5: "qf8", 8: "kv8", 15: "kv3", 17: "kv4", 20: "kv5", 21: "kv6", 22: "kv7"})
+    for c in range(4, 24):
+        vector += ["s%d" % c, between.get(c)]
+    return {"D": vector, "A": scalar, "P": tensor, "G": gpsimd, "S": ["load", "mo", "cd", "mi", "store"]}
+
+
 SCRATCH = {
     "St0": ("sbuf", [128, WIN], "bfloat16"), "St1": ("sbuf", [128, WIN], "bfloat16"),
     "UPS": ("sbuf", [128, UPW], "int32"), "FR": ("sbuf", [128, 10], "int32"),
     "OG": ("sbuf", [128, 3072], "bfloat16"), "CM": ("sbuf", [128, 3072], "bfloat16"), "OF": ("sbuf", [128, 3072], "bfloat16"),
-    "LF": ("sbuf", [128, 16], "float32"), "LP": ("sbuf", [128, 16], "uint16"),
-    "PQ": ("sbuf", [128, 192], "uint16"), "QF": ("sbuf", [128, 192], "float32"), "OX": ("sbuf", [128, 192], "uint16"),
-    "PK": ("sbuf", [128, RO * SLOT], "bfloat16"), "LAND": ("sbuf", [128, RO * D * SLOT], "bfloat16"),
-    "XG": ("sbuf", [128, 160], "bfloat16"),
-    "XT0": ("sbuf", [128, 128], "bfloat16"), "XT1": ("sbuf", [128, 128], "bfloat16"),
-    "XT2": ("sbuf", [128, 128], "bfloat16"), "XT3": ("sbuf", [128, 128], "bfloat16"),
-    "MB": ("sbuf", [128, 10 * PW], "bfloat16"), "CC": ("sbuf", [128, 10 * PW], "bfloat16"), "PC": ("sbuf", [128, 10 * PW], "bfloat16"),
-    "FL": ("sbuf", [128, 6 * PW], "bfloat16"), "RS": ("sbuf", [128, 6 * PW], "bfloat16"),
-    "EI": ("sbuf", [128, 1536], "bfloat16"), "ES": ("sbuf", [128, 1536], "bfloat16"), "HB": ("sbuf", [128, 256], "bfloat16"),
-    "TI": ("sbuf", [128, 32], "float32"), "TR": ("sbuf", [128, 32], "bfloat16"), "XF": ("sbuf", [128, 192], "float32"),
-    "II": ("sbuf", [128, 128], "bfloat16"), "ID": ("sbuf", [128, 128], "bfloat16"), "IDF": ("sbuf", [128, 128], "float32"),
-    "IZ": ("sbuf", [128, 128], "bfloat16"), "DP": ("sbuf", [128, 256], "bfloat16"),
-    "Z": ("sbuf", [128, 144], "bfloat16"), "T8": ("sbuf", [128, 16], "bfloat16"), "ONE": ("sbuf", [128, 512], "bfloat16"),
-    "SI": ("sbuf", [128, 256], "float32"), "SEL": ("sbuf", [128, 256 * (RO - 1)], "bfloat16"), "MAG": ("sbuf", [128, 384], "bfloat16"),
+    "LF": ("sbuf", [128, 16], "float32"), "LP": ("sbuf", [128, 12], "uint16"), "PQ": ("sbuf", [128, 192], "uint16"),
+    "QF": ("sbuf", [128, 192], "float32"), "XF": ("sbuf", [128, 192], "float32"), "OX": ("sbuf", [128, 192], "uint16"),
+    "XS": ("sbuf", [128, RO * XW], "bfloat16"), "LAND": ("sbuf", [128, RO * D * SLOT], "bfloat16"),
+    "XT": ("sbuf", [128, 128 * len(TILES)], "bfloat16"),
+    "CC": ("sbuf", [128, 10 * PW], "bfloat16"), "PC": ("sbuf", [128, 10 * PW], "bfloat16"),
+    "FL": ("sbuf", [128, 3 * PW], "bfloat16"), "RS": ("sbuf", [128, 6 * PW], "bfloat16"),
+    "MK": ("sbuf", [128, 200], "bfloat16"), "MC": ("sbuf", [128, 200], "bfloat16"),
+    "EI": ("sbuf", [128, 512], "bfloat16"), "SH": ("sbuf", [128, 384], "bfloat16"), "ES": ("sbuf", [128, 1536], "bfloat16"), "E1": ("sbuf", [128, 256], "bfloat16"),
+    "II": ("sbuf", [128, 128], "bfloat16"), "ID": ("sbuf", [128, 128], "bfloat16"), "IZ": ("sbuf", [128, 128], "bfloat16"),
+    "HB": ("sbuf", [128, 128 * (RO + 1)], "bfloat16"), "DP": ("sbuf", [128, 256], "bfloat16"),
+    "TI": ("sbuf", [128, 32], "float32"), "TR": ("sbuf", [128, 32], "bfloat16"),
+    "Z": ("sbuf", [128, 288], "bfloat16"), "T8": ("sbuf", [128, 16], "bfloat16"), "ONE": ("sbuf", [128, 512], "bfloat16"),
+    "SI": ("sbuf", [128, 144], "bfloat16"), "SEL": ("sbuf", [128, 144 * (RO - 1)], "bfloat16"), "MAG": ("sbuf", [128, 128], "bfloat16"),
     "KI": ("sbuf", [128, 8], "int32"), "CF": ("sbuf", [128, 64], "float32"), "CB": ("sbuf", [128, 4], "bfloat16"),
 }
 for _i in range(8):
     SCRATCH["P%d" % _i] = ("psum", [128, 512], "float32")
-SEMAPHORES = (["sP", "sA", "sD", "sG", "dfr", "drec", "dy", "snt"] + ["dup%d" % i for i in range(6)]
+SEMAPHORES = (["sP", "sA", "sD", "sG", "dfr", "drec0", "drec1", "dy", "dmo", "dmi", "snt"] + ["dup%d" % i for i in range(6)]
               + ["arr%d" % w for w in range(RO)] + ["dcp%d" % w for w in range(RO)])
+ORDER = []
+
+
+def is_psum(buf):
+    return SCRATCH[buf][0] == "psum"
+
+
+def order_of(calls):
+    before, seen = [], {}
+    for n, c in enumerate(calls):
+        pre = set()
+        for acc, wr in ((c[1], False), (c[2], True)):
+            for buf, a, b in acc:
+                pre.update(m for a0, b0, wr0, m in seen.get(buf, []) if is_psum(buf) or (a0 < b and b0 > a and (wr or wr0)))
+        for acc, wr in ((c[1], False), (c[2], True)):
+            for buf, a, b in acc:
+                h = seen.setdefault(buf, [])
+                if wr or is_psum(buf):
+                    h[:] = [e for e in h if not (is_psum(buf) or (a <= e[0] and e[1] <= b))]
+                h.append((a, b, wr, n))
+        before.append(pre)
+    lines = {}
+    for w in range(RO):
+        for q, steps in plan(w).items():
+            lines.setdefault(q, []).extend(n for s in steps for n, c in enumerate(calls) if c[0] == q and c[3] == (w, s))
+    order, done = [], set()
+    while len(order) < len(calls):
+        had = len(order)
+        for line in lines.values():
+            while line and before[line[0]] <= done:
+                done.add(line[0])
+                order.append(line.pop(0))
+        assert len(order) > had, "the plan goes against the data flow"
+    return order
 
 
 def rank_program(g, core, T, topo):
@@ -52,195 +108,160 @@ def rank_program(g, core, T, topo):
     if rank is None:
         return
     queues = {"P": g.tensor, "A": g.scalar, "D": g.vector, "G": g, "S": g.sync}
-    count = {"P": 0, "A": 0, "D": 0, "G": 0}
-    know = {q: {} for q in queues}
-    hist = {}
-    dmas = []
+    vec, act, ten = g.vector, g.scalar, g.tensor
+    calls, now = [], [0, ""]
 
-    def deps(q, reads, writes):
-        found = []
-        for acc, wr in ((reads, False), (writes, True)):
-            for buf, a, b in acc:
-                psum = buf[0] == "P" and buf[1:].isdigit()
-                for e in hist.get(buf, []):
-                    if psum:
-                        if e[3] != q:
-                            found.append(e)
-                    elif e[0] < b and e[1] > a:
-                        if (e[2] and (CFG["waw"] or not wr or e[3] != q)) or (wr and e[3] != q):
-                            found.append(e)
-        k = know[q]
-        best = {}
-        for e in found:
-            if k.get(e[4], 0) >= e[5] or any(f is not e and f[6].get(e[4], 0) >= e[5] for f in found):
-                continue
-            best[e[4]] = max(best.get(e[4], 0), e[5])
-        for s, v in best.items():
-            queues[q].wait_ge(T.sem[s], v)
-        for e in found:
-            k[e[4]] = max(k.get(e[4], 0), e[5])
-            for s, v in e[6].items():
-                k[s] = max(k.get(s, 0), v)
+    def step(name, j=""):
+        now[1] = "%s%s" % (name, j)
 
-    def note(q, reads, writes, sem, val, snap):
-        for acc, wr in ((reads, False), (writes, True)):
-            for buf, a, b in acc:
-                h = hist.setdefault(buf, [])
-                if wr:
-                    h[:] = [e for e in h if not (a <= e[0] and e[1] <= b)]
-                else:
-                    h[:] = [e for e in h if not (not e[2] and e[3] == q and e[4] == sem and a <= e[0] and e[1] <= b)]
-                h.append((a, b, wr, q, sem, val, snap))
-
-    def run(q, reads, writes, f):
-        deps(q, reads, writes)
-        snap = dict(know[q])
-        count[q] += 1
-        f().then_inc(T.sem["s" + q], 1)
-        note(q, reads, writes, "s" + q, count[q], snap)
+    def run(q, reads, writes, f, *args, **kw):
+        calls.append((q, reads, writes, tuple(now), None, f, args, kw))
 
     def dma(q, sem, reads, writes, out, in_):
-        deps(q, reads, writes)
-        snap = dict(know[q])
-        queues[q].dma_start(out, in_).then_inc(T.sem[sem], 16)
-        note("dma" + sem, reads, writes, sem, 16, snap)
-        dmas.append(sem)
-
-    vec, act, ten = g.vector, g.scalar, g.tensor
+        calls.append((q, reads, writes, tuple(now), sem, queues[q].dma_start, (out, in_), {}))
 
     def ap(x, n=128, p0=0):
+        if not isinstance(x, tuple):
+            return x
         s = x[3] if len(x) > 3 else 1
         return T[x[0]][p0:p0 + n, x[1]:x[2]:s] if s != 1 else T[x[0]][p0:p0 + n, x[1]:x[2]]
 
     def rg(*xs):
         return [x[:3] for x in xs if isinstance(x, tuple)]
 
-    def val(x, n=128):
-        return ap(x, n) if isinstance(x, tuple) else x
-
     def memset(x, c, n=128, p0=0):
-        run("D", [], rg(x), lambda: vec.memset(ap(x, n, p0), c))
+        run("D", [], rg(x), vec.memset, ap(x, n, p0), c)
 
     def ts(out, in0, s1, s2, op0, op1=None, n=128):
-        if op1 is None:
-            run("D", rg(in0, s1), rg(out), lambda: vec.tensor_scalar(ap(out, n), ap(in0, n), val(s1, n), None, op0))
-        else:
-            run("D", rg(in0, s1, s2), rg(out), lambda: vec.tensor_scalar(ap(out, n), ap(in0, n), val(s1, n), val(s2, n), op0, op1))
+        run("D", rg(in0, s1, s2), rg(out), vec.tensor_scalar, ap(out, n), ap(in0, n), ap(s1, n), ap(s2, n), *[o for o in (op0, op1) if o is not None])
 
     def tt(out, a, b, op):
-        run("D", rg(a, b), rg(out), lambda: vec.tensor_tensor(ap(out), ap(a), ap(b), op))
+        run("D", rg(a, b), rg(out), vec.tensor_tensor, ap(out), ap(a), ap(b), op)
 
-    def cp(out, in_, n=128):
-        run("D", rg(in_), rg(out), lambda: vec.tensor_copy(ap(out, n), ap(in_, n)))
+    def cp(out, in_):
+        run("D", rg(in_), rg(out), vec.tensor_copy, ap(out), ap(in_))
 
     def scan(out, d0, d1, first, op0, op1):
-        run("D", rg(d0, d1, first), rg(out), lambda: vec.tensor_tensor_scan(ap(out), ap(d0), ap(d1), val(first), op0, op1))
+        run("D", rg(d0, d1, first), rg(out), vec.tensor_tensor_scan, ap(out), ap(d0), ap(d1), ap(first), op0, op1)
 
-    def actv(out, in_, f, bias=0.0, scale=1.0, n=128):
-        run("A", rg(in_, bias, scale), rg(out), lambda: act.activation(ap(out, n), ap(in_, n), f, bias=val(bias), scale=val(scale)))
+    def actv(out, in_, f=AF.Identity, bias=0.0, scale=1.0, n=128, p0=0):
+        run("A", rg(in_, bias, scale), rg(out), act.activation, ap(out, n, p0), ap(in_, n, p0), f, bias=ap(bias), scale=ap(scale))
 
     def mm(out, lhsT, rhs, start, stop, m=128, k=128):
-        run("P", rg(lhsT, rhs), rg(out), lambda: ten.matmul(ap(out, m), ap(lhsT, k), ap(rhs, k), start, stop))
+        run("P", rg(lhsT, rhs), rg(out), ten.matmul, ap(out, m), ap(lhsT, k), ap(rhs, k), start, stop)
 
     def iota(x, pat, base, cm, n=128):
-        if SCRATCH[x[0]][2] == "int32":
-            run("G", [], rg(x), lambda: g.iota(ap(x, n), pat, base, cm))
-        else:
-            run("G", [], rg(x), lambda: g.iota(ap(x, n), pat, base, cm, allow_small_or_imprecise_dtypes=True))
+        kw = {} if SCRATCH[x[0]][2] == "int32" else {"allow_small_or_imprecise_dtypes": True}
+        run("G", [], rg(x), g.iota, ap(x, n), pat, base, cm, **kw)
 
     def sel(out, in_, pat, op, base, cm):
-        run("G", rg(in_), rg(out), lambda: g.affine_select(ap(out), ap(in_), pat, op, 0.0, base, cm))
+        run("G", rg(in_), rg(out), g.affine_select, ap(out), ap(in_), pat, op, 0.0, base, cm)
 
-    def gcopy(out, in_, n):
-        sel(out, in_, [[0, n]], OP.is_ge, 1, 0)
+    def gcopy(out, in_):
+        sel(out, in_, [[0, out[2] - out[1]]], OP.is_ge, 1, 0)
 
+    def by(window, offsets):
+        return ap(window).indirect(ap(offsets))
+
+    step("fr")
     dma("A", "dfr", [], [("FR", 0, 10)], T.FR[:], T.fr[:])
-    dma("S", "drec", [], [("St0", 0, V)], T.St0[:, 0:V], T.rec[:])
-    dma("A", "dup0", [], [("UPS", 0, 640)], T.UPS[:, 0:640], T.up[:, 0:640])
-    for i in range(1, 5):
-        dma("S", "dup%d" % i, [], [("UPS", 640 * i, 640 * i + 640)], T.UPS[:, 640 * i:640 * i + 640], T.up[:, 640 * i:640 * i + 640])
-    dma("S", "dup5", [], [("UPS", GH, GH + 640)], T.UPS[:, GH:GH + 640], T.up[:, V:V + 640])
+    step("load")
+    for j, (a, b) in enumerate(PIECES):
+        dma("S", "drec%d" % j, [], [("St0", a, b)], T.St0[:, a:b], T.rec[:, a:b])
+    for i in range(6):
+        a = 640 * i if i < 5 else GH
+        step("load" if i else "up_0")
+        dma("S" if i else "A", "dup%d" % i, [], [("UPS", a, a + 640)], T.UPS[:, a:a + 640], T.up[:, 640 * i:640 * i + 640])
 
-    C = {n: ("CF", j, j + 1) for j, n in enumerate(["p", "m0", "p160", "r", "scol", "obias", "nr", "t", "zc", "own", "ghost", "thr"])}
-    SC = [("CF", 12 + w, 13 + w) for w in range(RO)]
-    BASE = ("CF", 36, 46)
-    CAP, GB = ("CB", 0, 1), ("CB", 2, 4)
+    C = {n: ("CF", j, j + 1) for j, n in enumerate(["p", "m0", "p160", "r", "scol", "nr", "t", "zs", "zb", "own", "ghost", "thr", "drop"])}
+    HC = [("CF", 14 + w, 15 + w) for w in range(RO)]
+    BASE, CAP, GB = ("CF", 36, 46), ("CB", 0, 1), ("CB", 2, 4)
+    NT = 128 * len(TILES)
+
+    def line(out, a, b):
+        actv(out, C["r"], bias=float(a), scale=float(b - a))
+
+    step("kg0")
     iota(("KI", 0, 1), [[0, 1]], 0, 1)
     iota(("CF", 20, 30), [[320, 10]], 0, 0)
     iota(("II", 0, 128), [[-1, 128]], 0, 1)
     iota(("EI", 0, 512), [[-1, 32], [0, 16]], 0, 1, n=96)
-    memset(("ONE", 0, 512), 1.0)
-    memset(("MAG", 256, 384), WHOLE, n=1)
     iota(("TI", 0, 32), [[0, 4], [16, 8]], 0, 0)
-    sel(("T8", 0, 8), ("ONE", 0, 8), [[-16, 8]], OP.is_ge, 0, 1)
-    sel(("T8", 8, 16), ("T8", 0, 8), [[16, 8]], OP.is_ge, 15, -1)
-    iota(("EI", 512, 1536), [[-1, 64], [0, 16]], -32, 1, n=96)
-    memset(("St0", V, SW), 0.0)
-    memset(("St1", V, SW), 0.0)
-    memset(("MAG", 0, 128), COARSE, n=1)
-    memset(("MAG", 128, 256), -COARSE, n=1)
-    memset(("Z", 0, 144), 0.0)
-    for x in ("XT0", "XT1", "XT2", "XT3"):
-        memset((x, 0, 128), 0.0, n=96)
-        memset((x, 0, 128), 1.0, n=1, p0=96)
+    step("kv0")
+    memset(("ONE", 0, 512), 1.0)
+    memset(("XT", 0, NT), 0.0, n=96)
     ts(("KI", 1, 2), ("KI", 0, 1), 3, 1, OP.logical_shift_right, OP.bitwise_and)
     ts(("KI", 2, 3), ("KI", 0, 1), 7, None, OP.bitwise_and)
     ts(("KI", 3, 4), ("KI", 0, 1), 15, None, OP.bitwise_and)
-    for x in ("XT0", "XT1", "XT2", "XT3"):
-        run("D", [(x, 0, 128)], [(x, 0, 128)], lambda: vec.memset(T[x][96:97, 15:128:16], 0.0))
+    memset(("St0", V, SW), 0.0)
     ts(C["p160"], ("KI", 1, 2), 160.0, None, OP.mult)
     ts(C["r"], ("KI", 3, 4), 15.0, None, OP.is_equal)
     cp(C["p"], ("KI", 1, 2))
+    cp(C["t"], ("KI", 3, 4))
+    ts(("ID", 0, 128), ("II", 0, 128), 0.0, None, OP.is_equal)
+    ts(BASE, ("CF", 20, 30), C["p160"], None, OP.add)
+    memset(("XT", 0, NT), 1.0, n=1, p0=96)
+    memset(("MAG", 0, 128), WHOLE, n=1)
+    memset(("Z", 0, 288), 0.0)
+    memset(("St1", V, SW), 0.0)
+    memset(("XT", 15, NT, 16), 0.0, n=1, p0=96)
+    memset(("MAG", 15, 128, 16), 0.0, n=1)
+    step("kg0")
+    sel(("T8", 0, 8), ("ONE", 0, 8), [[-16, 8]], OP.is_ge, 0, 1)
+    sel(("T8", 8, 16), ("T8", 0, 8), [[16, 8]], OP.is_ge, 15, -1)
+    step("ks0")
+    actv(("ES", 0, 512), ("ONE", 0, 512), scale=-0.25, n=1, p0=96)
+    line(C["scol"], 1, -1)
+    line(C["nr"], 1, 0)
+    line(C["drop"], -WHOLE, 1)
+    line(C["zs"], -STEP, SHIFT)
+    line(C["zb"], -2 * STEP, SHIFT + 15 * STEP)
+    for w in range(RO):
+        line(HC[w], 0.5, tag(w) if w < RO - 1 else 0.0)
+    actv(("IZ", 0, 128), ("ID", 0, 128), scale=C["nr"])
+    actv(("HB", 0, 128), ("ID", 0, 128), scale=-0.5)
+    actv(("HB", 128, 256), ("ID", 0, 128), scale=HC[0])
+    step("ks1")
+    actv(("TR", 0, 32), ("TI", 0, 32), bias=C["t"])
+    actv(("Z", 15, 128, 16), ("T8", 8, 16), scale=C["zs"])
+    actv(("Z", 144 + 15, 144 + 128, 16), ("T8", 8, 16), scale=C["zb"])
+    step("kv1")
+    ts(("ES", 0, 512), ("EI", 0, 512), 0.0, 0.5, OP.is_equal, OP.mult, n=96)
+    ts(("E1", 0, 256), ("EI", 0, 256), 0.0, None, OP.is_equal, n=96)
+    for j in (1, 2):
+        step("kv1")
+        ts(("SH", 128 * j, 128 * j + 128), ("II", 0, 128), -32.0 * j, None, OP.is_equal, n=96)
+        run("D", [("ID", 0, 128)], [("SH", 128 * j, 128 * j + 128)], vec.tensor_copy, T.SH[96:97, 128 * j:128 * j + 128], T.ID[96:97, 0:128])
+        step("kp")
+        mm(("P%d" % (4 + j), 0, 512), ("SH", 128 * j, 128 * j + 97), ("ES", 0, 512), True, True, m=97, k=97)
+        step("ks2")
+        actv(("ES", 512 * j, 512 * j + 512), ("P%d" % (4 + j), 0, 512), AF.Copy, n=97)
+    step("ks3")
+    line(CAP, 255, 1)
+    actv(C["m0"], C["p"], bias=1.0, scale=-1.0)
+    actv(GB, ("CF", 36, 38))
+    actv(("DP", 0, 128), ("ID", 0, 128), scale=C["m0"])
+    actv(("DP", 128, 256), ("ID", 0, 128), scale=C["p"])
+    step("ks4")
+    for w in range(1, RO):
+        actv(("HB", 128 * w + 128, 128 * w + 256), ("ID", 0, 128), scale=HC[w])
+    step("kv2")
     ts(C["own"], ("KI", 2, 3), float(V), None, OP.add)
     ts(C["ghost"], ("KI", 2, 3), float(D * B), None, OP.add)
     ts(C["thr"], ("KI", 2, 3), BIG, BIG, OP.mult, OP.add)
-    ts(BASE, ("CF", 20, 30), C["p160"], None, OP.add)
-    ts(C["scol"], C["r"], -2.0, 1.0, OP.mult, OP.add)
-    ts(C["nr"], C["r"], -1.0, 1.0, OP.mult, OP.add)
-    ts(CAP, C["r"], -254.0, 255.0, OP.mult, OP.add)
-    ts(C["m0"], C["p"], -1.0, 1.0, OP.mult, OP.add)
-    if CFG["tr"]:
-        ts(C["zc"], C["r"], float(SHIFT + STEP), -float(STEP), OP.mult, OP.add)
-    else:
-        ts(C["zc"], C["r"], 2304.0 + 128.0, -128.0, OP.mult, OP.add)
-    ts(C["obias"], C["r"], WHOLE + 1, -WHOLE, OP.mult, OP.add)
-    cp(C["t"], ("KI", 3, 4))
-    memset(("MAG", 256 + 15, 384, 16), 0.0, n=1)
-    cp(GB, ("CF", 36, 38))
-    ts(("ID", 0, 128), ("II", 0, 128), 0.0, None, OP.is_equal)
-    ts(("HB", 0, 128), ("II", 0, 128), 0.0, 0.5, OP.is_equal, OP.mult)
-    ts(("HB", 128, 256), ("II", 0, 128), 0.0, -0.5, OP.is_equal, OP.mult)
-    ts(("TR", 0, 32), ("TI", 0, 32), C["t"], None, OP.add)
-    for w in range(RO):
-        ts(SC[w], C["r"], 2 * tag(w) if w < RO - 1 else 0.0, C["nr"], OP.mult, OP.add)
-    ts(("IZ", 0, 128), ("II", 0, 128), 0.0, C["nr"], OP.is_equal, OP.mult)
-    ts(("IDF", 0, 128), ("II", 0, 128), 0.0, None, OP.is_equal)
-    run("D", [("T8", 8, 16), C["zc"], ("Z", 0, 144)], [("Z", 0, 144)],
-        lambda: vec.tensor_scalar(T.Z[:, 15:128:16], T.T8[:, 8:16], ap(C["zc"]), None, OP.mult))
-
-    def spreads(a, b):
-        memset(("ES", a, b), -0.25, n=1, p0=96)
-        ts(("ES", a, b), ("EI", a, b), 0.0, 0.5, OP.is_equal, OP.mult, n=96)
-
-    spreads(0, 512)
-
-    def late_gpsimd():
-        iota(("UPS", V, V + 16), [[16, 16]], V, 1)
-        iota(("UPS", GH + D * B, UPW), [[16, 16]], V, 1)
-        iota(("SI", 0, 128), [[-16, 8], [-1000, 2], [0, 8]], -15, 1)
-        iota(("SI", 128, 256), [[-16, 8], [-1000, 2], [0, 8]], 985, 1)
-        iota(("FL", 0, 6 * PW), [[0, 6], [1, PW]], 0, 0)
-
-    def late_vector():
-        ts(("DP", 0, 128), ("II", 0, 128), 0.0, C["m0"], OP.is_equal, OP.mult)
-        ts(("DP", 128, 256), ("II", 0, 128), 0.0, C["p"], OP.is_equal, OP.mult)
-        memset(("RS", 0, 6 * PW), 0.0)
-
-    def later_vector():
-        run("D", [("RS", 0, 6 * PW)], [("RS", 0, 6 * PW)], lambda: vec.memset(T.RS[:, B:6 * PW:PW], 2.0 ** 20))
-        for w in range(RO - 1):
-            ts(("SEL", 256 * w, 256 * w + 256), ("SI", 0, 256), 0.0, -BIG / tag(w), OP.is_equal, OP.mult)
-        ts(("FL", B, 6 * PW, PW), ("ONE", 0, 6), C["thr"], None, OP.mult)
+    memset(("RS", 0, 6 * PW), 0.0)
+    step("kv8")
+    memset(("RS", B, 6 * PW, PW), 2.0 ** 20)
+    step("kg1")
+    iota(("UPS", V, V + 16), [[16, 16]], V, 1)
+    iota(("UPS", GH + D * B, UPW), [[16, 16]], V, 1)
+    iota(("SI", 0, 144), [[-16, 9], [-1000, 2], [0, 8]], 985, 1)
+    iota(("FL", 0, 3 * PW), [[0, 3], [1, PW]], 0, 0)
+    for w in range(RO - 1):
+        step("kv", 3 + w)
+        ts(("SEL", 144 * w, 144 * w + 144), ("SI", 0, 144), 0.0, -BIG / tag(w), OP.is_equal, OP.mult)
+    step("kv7")
+    ts(("FL", B, 3 * PW, PW), ("ONE", 0, 3), C["thr"], None, OP.mult)
 
     dests = [T.cores[(rank + d) % 8] for d in range(1, D + 1)]
     pick, used = {}, set()
@@ -249,279 +270,220 @@ def rank_program(g, core, T, topo):
         used.update(e)
         pick[dst] = sum(1 << x for x in e)
 
-    CH = [(0, 1, "XT0", 0), (1, 2, "XT0", 16), (2, 4, "XT1", 0), (4, 6, "XT2", 0), (6, 8, "XT2", 32), (8, 10, "XT2", 64), (10, 12, "XT3", 0)]
-    NC = len(CH)
     for w in range(RO):
+        now[0] = w
         X, Y = "St%d" % (w % 2), "St%d" % ((w + 1) % 2)
-        pk = SLOT * w
+        xs, land = XW * w, SLOT * D * w
 
-        def gather_up(c0, c1, a0, a1):
-            a, b = 16 * c0, 16 * c1
-            run("D", [("LP", c0, c1), ("UPS", a0, a1)], [("PQ", a, b)],
-                lambda: vec.tensor_copy(T.PQ[:, a:b], T.UPS[:, a0:a1].indirect(T.LP[:, c0:c1])))
+        def notes(c0, c1):
+            return ("XS", xs + 16 + 16 * c0, xs + 16 + 16 * c1)
 
-        def qf(c0, c1):
-            cp(("QF", 16 * c0, 16 * c1), ("PQ", 16 * c0, 16 * c1))
+        def parents(c0, c1, window):
+            pq = ("PQ", 16 * c0, 16 * c1)
+            step("up", c0)
+            run("D", [("LP", c0, c1), window], [pq], vec.tensor_copy, ap(pq), by(window, ("LP", c0, c1)))
+            step("qf", c0)
+            cp(("QF", 16 * c0, 16 * c1), pq)
 
-        def gather_x(out, c0, c1):
-            run("A", [("LP", c0, c1), (X, 0, SW)], rg(out),
-                lambda: act.activation(ap(out), T[X][:, 0:SW].indirect(T.LP[:, c0:c1]), AF.Copy))
+        def gather_x(c0, c1):
+            step("x", c0)
+            window = (X, 0, SW if w else 320 * c1)
+            run("A", [("LP", c0, c1), window], [notes(c0, c1)], act.activation, ap(notes(c0, c1)), by(window, ("LP", c0, c1)), AF.Copy)
 
-        def edges(buf, i, per=256):
-            return (buf, per * CH[i][0], per * CH[i][1])
-
-        def gather_old(i):
-            run("A", [edges("PQ", i, 16), (X, 0, SW), C["scol"], C["r"]], [edges("OG", i)],
-                lambda: act.activation(ap(edges("OG", i)), T[X][:, 0:SW].indirect(ap(edges("PQ", i, 16))), AF.Relu,
-                                       bias=ap(C["r"]), scale=ap(C["scol"])))
-
-        def bank(i, first):
-            return ("P%d" % (first + i % 2), 0, 256 * (CH[i][1] - CH[i][0]))
-
-        def spread(i, first, k):
-            a = 16 * CH[i][3]
-            mm(bank(i, first), (CH[i][2], 0, 128), ("ES", a, a + bank(i, first)[2]), True, False, k=k)
-
-        def less(i):
-            spread(i, 3, 97)
-
-        def olds(i):
-            mm(bank(i, 3), ("HB", 128, 256), edges("OG", i), False, True)
-
-        def total(i):
-            spread(i, 5, 97)
-            mm(bank(i, 5), ("HB", 0, 128), edges("OG", i), False, False)
-            mm(bank(i, 5), ("MAG", 256, 384), ("ONE", 0, bank(i, 5)[2]), False, True, k=1)
-
-        def signs(i):
-            actv(edges("CM", i), bank(i, 3), AF.Sign, bias=0.125, scale=-1.0)
-
-        def offers(i, a=0, b=None):
-            o, s = edges("OF", i), bank(i, 5)
-            b = s[2] if b is None else b
-            if i in CFG["vof"]:
-                ts(("OF", o[1] + a, o[1] + b), (s[0], a, b), SC[w], C["obias"], OP.mult, OP.add)
+        cv, cs, cg = CFG["cv"], CFG["cs"], CFG["cg"]
+        if w == 0:
+            for j, (a, b) in enumerate(((0, 640), (640, 1600), (1600, V))):
+                step("cv", j)
+                cp((Y, a, b), (X, a, b))
+        else:
+            step("cv0")
+            ts((Y, 0, cv), (X, 0, cv), CAP, None, OP.min)
+            if w < RO - 1:
+                a = cv + cs + cg
+                step("cs")
+                actv((Y, cv, cv + cs), (X, cv, cv + cs), AF.Copy)
+                step("cd")
+                dma("S", "dcp%d" % w, [(X, a, V)], [(Y, a, V)], T[Y][:, a:V], T[X][:, a:V])
             else:
-                actv(("OF", o[1] + a, o[1] + b), (s[0], a, b), AF.Identity, bias=C["obias"], scale=SC[w])
+                a = cv + cs // 2
+                step("cs")
+                actv(("OF", cv, a), (X, cv, a), AF.Relu, bias=C["r"], scale=C["scol"])
+                actv((Y, cv, a), ("OF", cv, a), bias=C["r"], scale=C["scol"])
+                n = (V - a) // 16
+                step("mo")
+                dma("S", "dmo", [(X, a, V)], [("MK", 0, n)], T.MK[:, 0:n], T[X][15:128:16, a:V])
+                step("cd")
+                for j in range(8):
+                    dma("S", "dcp%d" % w, [(X, a, V)], [(Y, a + 16 * j, a + 16 * j + 16)], T[Y][16 * j:16 * j + 15, a:V], T[X][16 * j:16 * j + 15, a:V])
+                step("cap")
+                ts(("MC", 0, n), ("MK", 0, n), 1.0, None, OP.min)
+                step("mi")
+                dma("S", "dmi", [("MC", 0, n)], [(Y, a + 128, V)], T[Y][15:128:16, a:V], T.MC[:, 0:n])
 
-        def cbank(i):
-            return ("P%d" % (1 + i % 2), 0, 16 * (CH[i][1] - CH[i][0]))
-
-        def count_open(i):
-            if CFG["tr"]:
-                mm(cbank(i), ("ID", 0, 128), ("TR", 0, cbank(i)[2]), True, False)
-            else:
-                mm(cbank(i), ("MAG", 0, 128), ("ONE", 0, cbank(i)[2]), True, False, k=1)
-
-        def counts(i):
-            _, a, b = edges("CM", i)
-            for t in range(16):
-                mm(cbank(i), ("Z", 15 - t, 143 - t), ("CM", a + t, b, 16), False, CFG["tr"] and t == 15)
-            if not CFG["tr"]:
-                mm(cbank(i), ("MAG", 128, 256), ("ONE", 0, cbank(i)[2]), False, False, k=1)
-                mm(cbank(i), ("IDF", 0, 128), edges("QF", i, 16), False, True)
-
-        def targets(i):
-            if CFG["tr"]:
-                tt(edges("XF", i, 16), cbank(i), edges("QF", i, 16), OP.max)
-                cp(edges("OX", i, 16), edges("XF", i, 16))
-            else:
-                cp(edges("OX", i, 16), cbank(i))
-
-        def scatter(i):
-            for c in range(2 * CH[i][0], 2 * CH[i][1]):
-                run("D", [("OX", 8 * c, 8 * c + 8), ("OF", 128 * c, 128 * c + 128)], [(Y, 0, WIN)],
-                    lambda: vec.tensor_copy(T[Y][:, 0:WIN].indirect(T.OX[:, 8 * c:8 * c + 8]), T.OF[:, 128 * c:128 * c + 128]))
-
-        def marks(pb, c0, c1):
-            for c in range(c0, c1):
-                for p in (0, 1):
-                    b, s = 2 * c + p, 256 * (w - 1) + 128 * p
-                    mm((pb, PW * (c - c0), PW * (c - c0 + 1)), ("SEL", s, s + 128), (X, B * b, B * b + PW), p == 0, p == 1)
-
-        def mcopy(pb, c0, c1):
-            actv(("MB", PW * c0, PW * c1), (pb, 0, PW * (c1 - c0)), AF.Copy)
-
-        def remaining(pb, c0, c1):
-            a, b = PW * c0, PW * c1
-            scan(("CC", a, b), (pb, 0, b - a) if pb != "MB" else (pb, a, b), ("FL", 0, b - a), C["thr"], OP.add, OP.max)
-
-        def places(c0, c1):
-            a, b = PW * c0, PW * c1
-            scan(("PC", a, b), ("RS", 0, b - a), ("CC", a, b), 2.0 ** 20, OP.add, OP.min)
-
-        def lists(c0, c1):
-            if c1 - c0 <= 2:
+        if w == 0:
+            step("first")
+            tt(("LF", 0, 10), ("FR", 0, 10), BASE, OP.add)
+            cp(("XS", xs + 14, xs + 16), ("FR", 0, 2))
+            for c0, c1 in LISTS:
+                step("li", c0)
+                cp(("LP", c0, c1), ("LF", c0, c1))
+                gather_x(c0, c1)
+                for c in range(c0, c1, 2):
+                    parents(c, c + 2, ("UPS", 0, 320 * c + 640))
+        else:
+            for c0, c1, pb in SCANS:
+                src = (pb, 0, PW * (c1 - c0))
                 for c in range(c0, c1):
-                    ts(("LP", c, c + 1), ("PC", PW * c + B - 1, PW * c + B), ("CF", 36 + c, 37 + c), C["own"], OP.add, OP.min)
-            else:
-                tt(("LF", c0, c1), ("PC", PW * c0 + B - 1, PW * c1, PW), ("CF", 36 + c0, 36 + c1), OP.add)
-                ts(("LP", c0, c1), ("LF", c0, c1), C["own"], None, OP.min)
+                    step("mk", c)
+                    for p in (0, 1):
+                        b, s = 2 * c + p, 144 * (w - 1) + 8 - 8 * p
+                        mm((pb, PW * (c - c0), PW * (c - c0 + 1)), ("SEL", s, s + 128), (X, B * b, B * b + PW), p == 0, p == 1)
+                step("rem", c0)
+                scan(("CC", PW * c0, PW * c1), src, ("FL", 0, src[2]), C["thr"], OP.add, OP.max)
+            for c0, c1 in LISTS:
+                a, b = PW * c0, PW * c1
+                for x, y in ((0, 1), (1, 2)) if c0 == 0 else ((c0, c1),):
+                    step("pl", x)
+                    scan(("PC", PW * x, PW * y), ("RS", 0, PW * (y - x)), ("CC", PW * x, PW * y), 2.0 ** 20, OP.add, OP.min)
+                if c1 - c0 <= 2:
+                    for c in range(c0, c1):
+                        step("li", c)
+                        ts(("LP", c, c + 1), ("PC", PW * c + B - 1, PW * c + B), ("CF", 36 + c, 37 + c), C["own"], OP.add, OP.min)
+                else:
+                    step("lf", c0)
+                    tt(("LF", c0, c1), ("PC", a + B - 1, b, PW), ("CF", 36 + c0, 36 + c1), OP.add)
+                    step("li", c0)
+                    ts(("LP", c0, c1), ("LF", c0, c1), C["own"], None, OP.min)
+                parents(c0, c1, ("UPS", 0, GH))
+                gather_x(c0, c1)
+            step("pk")
+            run("G", [("PC", B - 1, 2 * PW)], [("XS", xs + 14, xs + 16)], g.affine_select, T.XS[:, xs + 14:xs + 16], T.PC[:, B - 1:2 * PW:PW],
+                [[0, 2]], OP.is_ge, 0.0, 1, 0)
 
-        def xt(pb, col, src):
-            mm((pb, col, col + 128), src, ("IZ", 0, 128), True, True, m=src[2] - src[1])
+        step("send")
+        calls.append(("G", [("XS", xs + 14, xs + 48)], [("LAND", land, land + SLOT * D)], tuple(now), "arr%d" % w, g.remote_dma_fused, ([RemoteDMATransfer(
+            dst_ids=[DstId(rid=topo.addr(dst)[0], pnc=topo.addr(dst)[1])], dma_engine_mask=pick[dst], remote_sem=T.sem["arr%d" % w],
+            src=T.XS[:, xs + 14:xs + 48], dst=T.LAND[:, land + SLOT * d + 14:land + SLOT * d + 48]) for d, dst in enumerate(dests)],),
+            {"local_sem": T.sem.snt}))
 
-        def xtcopy(out, pb, col, n):
-            actv((out, 0, 128), (pb, col, col + 128), AF.Copy, n=n)
-
-        def send():
-            deps("G", [("PK", pk, pk + PKW)], [])
-            g.remote_dma_fused([RemoteDMATransfer(
-                dst_ids=[DstId(rid=topo.addr(dst)[0], pnc=topo.addr(dst)[1])], dma_engine_mask=pick[dst], remote_sem=T.sem["arr%d" % w],
-                src=T.PK[:, pk:pk + PKW], dst=T.LAND[:, SLOT * (D * w + d):SLOT * (D * w + d) + PKW]) for d, dst in enumerate(dests)],
-                local_sem=T.sem.snt)
-            note("R", [], [("LAND", SLOT * D * w, SLOT * D * (w + 1))], "arr%d" % w, 2 * D, {})
-
-        def ghost_notes():
+        def ghosts():
+            step("gn")
             for d in range(D):
-                s = SLOT * (D * w + d) + 8 * d
-                gcopy(("XG", 128 + 8 * d, 136 + 8 * d), ("LAND", s, s + 8), 8)
-
-        def ghost_places():
+                s = land + SLOT * d + 16 + 8 * d
+                gcopy(("XS", xs + 176 + 8 * d, xs + 184 + 8 * d), ("LAND", s, s + 8))
+            step("gp")
             for p in (0, 1):
-                s = SLOT * (D * w + p) + 32
+                s = land + SLOT * p + 14
                 mm(("P0", 384, 386), ("DP", 128 * p, 128 * p + 128), ("LAND", s, s + 2 * SLOT + 2, 2 * SLOT + 1), p == 0, False)
             mm(("P0", 384, 386), ("ID", 0, 128), GB, False, True)
-
-        def ghost_lists():
+            step("li", 10)
             ts(("LP", 10, 12), ("P0", 384, 386), C["ghost"], None, OP.min)
-            gather_up(10, 12, GH, UPW)
+            parents(10, 12, ("UPS", GH, UPW))
 
-        def capped(a, b):
-            ts((Y, a, b), (X, a, b), CAP, None, OP.min)
+        for i, (c0, c1) in enumerate(CHUNKS):
+            j, (t0, t1, pb) = [(j, t) for j, t in enumerate(TILES) if t[0] <= c0 < t[1]][0]
+            tile = ("XT", 128 * j, 128 * j + 128)
+            if c0 == t0:
+                if t1 > 10:
+                    ghosts()
+                step("xt", j)
+                mm((pb, 0, 128), notes(t0, t1), ("IZ", 0, 128), True, True, m=16 * (t1 - t0))
+                step("xc", j)
+                actv(tile, (pb, 0, 128), AF.Copy, n=16 * (t1 - t0))
+            n = 256 * (c1 - c0)
+            og, cm, of = [(buf, 256 * c0, 256 * c1) for buf in ("OG", "CM", "OF")]
+            pq, qf, xf, ox = [(buf, 16 * c0, 16 * c1) for buf in ("PQ", "QF", "XF", "OX")]
+            pc, pd, ps = ("P%d" % (1 + i % 2), 0, n // 16), ("P%d" % (3 + i % 2), 0, n), ("P%d" % (5 + i % 2), 0, n)
+            spread = ("ES", 256 * (c0 - t0), 256 * (c1 - t0))
+            step("G", i)
+            run("A", [pq, (X, 0, SW), C["scol"], C["r"]], [og],
+                act.activation, ap(og), by((X, 0, SW), pq), AF.Relu, bias=ap(C["r"]), scale=ap(C["scol"]))
+            step("dx", i)
+            if i == 0:
+                mm(pd, tile, ("E1", 0, n), True, True, k=96)
+                step("S", i)
+                tt(cm, og, pd, OP.is_ge)
+            else:
+                mm(pd, tile, spread, True, False, k=97)
+                step("do", i)
+                mm(pd, ("HB", 0, 128), og, False, True)
+                step("S", i)
+                actv(cm, pd, AF.Sign, bias=0.125, scale=-1.0)
+            step("sx", i)
+            mm(ps, tile, spread, True, False, k=97)
+            step("so", i)
+            mm(ps, ("HB", 128 * w + 128, 128 * w + 256), og, False, False)
+            step("sm", i)
+            mm(ps, ("MAG", 0, 128), ("ONE", 0, n), False, True, k=1)
+            step("O", i)
+            actv(of, ps, bias=C["drop"])
+            step("op", i)
+            mm(pc, ("ID", 0, 128), ("TR", 0, n // 16), True, False)
+            step("ct", i)
+            z = 144 * (i == 0)
+            for t in range(16):
+                mm(pc, ("Z", z + 15 - t, z + 143 - t), ("CM", cm[1] + t, cm[2], 16), False, t == 15)
+            step("xf", i)
+            tt(xf, pc, qf, OP.max)
+            step("ox", i)
+            cp(ox, xf)
+            for c in range(2 * c0, 2 * c1):
+                step("s", c)
+                run("D", [("OX", 8 * c, 8 * c + 8), ("OF", 128 * c, 128 * c + 128)], [(Y, 0, WIN)],
+                    vec.tensor_copy, by((Y, 0, WIN), ("OX", 8 * c, 8 * c + 8)), T.OF[:, 128 * c:128 * c + 128])
 
-        if w == 0:
-            tt(("LF", 0, 10), ("FR", 0, 10), BASE, OP.add)
-            cp(("LP", 0, 10), ("LF", 0, 10))
-            cp(("PK", pk + 32, pk + 34), ("FR", 0, 2))
-            gather_up(0, 2, 0, 640)
-            qf(0, 2)
-        else:
-            cv, cs, cg = CFG["cv"], CFG["cs"], CFG["cg"]
-            marks("P0", 0, 2)
-            marks("P7", 2, 4)
-            marks("P5", 4, 7)
-            marks("P6", 7, 10)
-            capped(0, cv)
-            if w < RO - 1:
-                if cv + cs + cg < V:
-                    dma("S", "dcp%d" % w, [(X, cv + cs + cg, V)], [(Y, cv + cs + cg, V)], T[Y][:, cv + cs + cg:V], T[X][:, cv + cs + cg:V])
-                if cs:
-                    actv((Y, cv, cv + cs), (X, cv, cv + cs), AF.Copy)
-                if cg:
-                    gcopy((Y, cv + cs, cv + cs + cg), (X, cv + cs, cv + cs + cg), cg)
-            remaining("P0", 0, 2)
-            places(0, 2)
-            lists(0, 2)
-            if CFG["mb"]:
-                mcopy("P7", 2, 4)
-            gcopy(("PK", pk + 32, pk + 34), ("PC", B - 1, 2 * PW, PW), 2)
-            gather_up(0, 2, 0, GH)
-
-        gather_x(("PK", pk, pk + 32), 0, 2)
-        xt("P0", 0, ("PK", pk, pk + 32))
-        send()
-        if w == 0:
-            late_gpsimd()
-        ghost_notes()
-        gather_old(0)
-        xtcopy("XT0", "P0", 0, 32)
-        count_open(0)
-        less(0)
-        olds(0)
-        if w > 0:
-            remaining("MB" if CFG["mb"] else "P7", 2, 4)
-            qf(0, 2)
-            places(2, 4)
-            remaining("P5", 4, 7)
-            lists(2, 4)
-            remaining("P6", 7, 10)
-            gather_up(2, 4, 0, GH)
-            places(4, 10)
-            qf(2, 4)
-            lists(4, 10)
-            if w == RO - 1:
-                capped(cv, V)
-        else:
-            spreads(512, 1536)
-            gather_up(2, 4, 0, 1280)
-            qf(2, 4)
-            capped(0, V)
-        gather_old(1)
-        less(1)
-        olds(1)
-        signs(0)
-        total(0)
-        counts(0)
-        count_open(1)
-        signs(1)
-        gather_x(("XG", 0, 32), 2, 4)
-        offers(0)
-        total(1)
-        xt("P7", 0, ("XG", 0, 32))
-        counts(1)
-        targets(0)
-        if w > 0:
-            gather_up(4, 10, 0, GH)
-        else:
-            gather_up(4, 6, 0, 1920)
-            qf(4, 6)
-        scatter(0)
-        gather_old(2)
-        xtcopy("XT1", "P7", 0, 32)
-        offers(1)
-        less(2)
-        olds(2)
-        total(2)
-        count_open(2)
-        targets(1)
-        if w > 0:
-            qf(4, 10)
-        else:
-            late_vector()
-        scatter(1)
-        gather_x(("XG", 32, 128), 4, 10)
-        xt("P7", 128, ("XG", 32, 128))
-        for i in range(2, NC):
-            if w == 0 and i < 4:
-                c = CH[i + 2][0]
-                gather_up(c, c + 2, 0, 320 * c + 640)
-                qf(c, c + 2)
-            signs(i)
-            if i == 2:
-                xtcopy("XT2", "P7", 128, 96)
-            counts(i)
-            if i in CFG["early"]:
-                offers(i)
-            if i + 1 < NC:
-                if i == 2:
-                    less(3)
-                gather_old(i + 1)
-                olds(i + 1)
-            if i == CFG["gh"]:
-                ghost_places()
-                xt("P0", 0, ("XG", 128, 160))
-            if i not in CFG["early"]:
-                offers(i)
-            if i == CFG["gh"]:
-                xtcopy("XT3", "P0", 0, 32)
-            if i + 1 < NC:
-                total(i + 1)
-                count_open(i + 1)
-            if i + 2 < NC:
-                less(i + 2)
-            targets(i)
-            if i == CFG["gh"]:
-                ghost_lists()
-            if i == CFG["gh"] + 1:
-                qf(10, 12)
-            if w == 0 and i == 4:
-                later_vector()
-            scatter(i)
-
+    step("store")
     dma("S", "dy", [("St%d" % (RO % 2), 0, V)], [], T.y[:], T["St%d" % (RO % 2)][:, 0:V])
-    for q in "PADG":
-        g.wait_ge(T.sem["s" + q], count[q])
-    for s in dmas:
-        g.wait_ge(T.sem[s], 16)
+
+    count = {"sP": 0, "sA": 0, "sD": 0, "sG": 0}
+    whole = {}
+    for c in calls:
+        whole[c[4]] = whole.get(c[4], 0) + 16
+    know = {q: {} for q in queues}
+    hist = {}
+    if not ORDER:
+        ORDER.extend(order_of(calls))
+    for n in ORDER:
+        q, reads, writes, _, sem, f, args, kw = calls[n]
+        remote = sem is not None and sem.startswith("arr")
+        found = []
+        for acc, wr in ((reads, False), ([] if remote else writes, True)):
+            for buf, a, b in acc:
+                for e in hist.get(buf, []):
+                    if is_psum(buf):
+                        if e[3] != q:
+                            found.append(e)
+                    elif e[0] < b and e[1] > a and (e[2] or (wr and e[3] != q)):
+                        found.append(e)
+        k, best = know[q], {}
+        for e in found:
+            if k.get(e[4], 0) >= e[5] or any(o is not e and o[6].get(e[4], 0) >= e[5] for o in found):
+                continue
+            best[e[4]] = max(best.get(e[4], 0), e[5])
+        for s, v in best.items():
+            queues[q].wait_ge(T.sem[s], v)
+        for e in found:
+            k[e[4]] = max(k.get(e[4], 0), e[5])
+            for s, v in e[6].items():
+                k[s] = max(k.get(s, 0), v)
+        snap = dict(k)
+        if remote:
+            f(*args, **kw)
+            who, value, reads, snap = "remote", 2 * D, [], {}
+        elif sem:
+            f(*args, **kw).then_inc(T.sem[sem], 16)
+            who, value = sem, whole[sem]
+            count[sem] = value
+        else:
+            sem = "s" + q
+            f(*args, **kw).then_inc(T.sem[sem], 1)
+            count[sem] += 1
+            who, value = q, count[sem]
+        for acc, wr in ((reads, False), (writes, True)):
+            for buf, a, b in acc:
+                h = hist.setdefault(buf, [])
+                h[:] = [e for e in h if not (a <= e[0] and e[1] <= b and (wr or (not e[2] and e[3] == who)))]
+                h.append((a, b, wr, who, sem, value, snap))
+    for s, v in count.items():
+        g.wait_ge(T.sem[s], v)
     g.wait_ge(T.sem.snt, 2 * D * RO)

import numpy as np
from concourse.bass import DstId, RemoteDMATransfer
from concourse.mybir import AluOpType as OP, ActivationFunctionType as AF

CFG = dict(cv=480, cs=800, cg=0)
V, NO, B, K, RO, D = 3200, 20, 160, 8, 5, 4
SW = V + 256
STEP, SHIFT = 1792, 5248
WIN = SHIFT + 15 * STEP + 128
GH = V + 16
UPW = GH + D * B + 16
WHOLE = 1.5 * 2.0 ** 23
BIG = 8192.0
PW = B + 1
XW, SLOT = 208, 48
PIECES = ((0, 640), (640, V))
SCANS = ((0, 1, "P0"), (1, 2, "P1"), (2, 4, "P7"), (4, 7, "P6"), (7, 10, "P2"))
LISTS = ((0, 2), (2, 4), (4, 10))
TILES = ((0, 2, "P0"), (2, 4, "P7"), (4, 10, "P7"), (10, 12, "P0"))
CHUNKS = ((0, 1), (1, 2), (2, 4), (4, 6), (6, 8), (8, 10), (10, 12))


def tag(w):
    return 2.0 ** (9 * (w + 1))


def plan(w):
    vector = ("cv0 rem0 rem1 pl0 pl1 li0 li1 rem2 up0 pl2 li2 li3 qf0 rem4 S0 cap rem7 up2 pl4 qf2 xf0 lf4 ox0 li4 "
              "s0 xf1 s1 ox1 up4 s2 s3 xf2 qf4 ox2").split()
    scalar = "cs x0 xc0 G0 G1 x2 O0 S1 xc1 G2 x4 O1 xc2 S2 G3 O2 S3 G4 O3 S4 G5 O4 S5 xc3 G6 O5 S6 O6".split()
    tensor = ("mk0 mk1 mk2 mk3 mk4 mk5 mk6 xt0 mk7 mk8 mk9 dx1 op0 dx0 sx0 so0 sm0 sx1 do1 xt1 ct0 so1 op1 sm1 ct1 "
              "dx2 xt2 do2 sx2 op2 so2 sm2 ct2 dx3 op3 do3 dx4 sx3 so3 sm3 ct3 do4 op4 sx4 so4 sm4 ct4 "
              "dx5 do5 gp sx5 so5 xt3 op5 ct5 sm5 dx6 do6 sx6 op6 so6 sm6 ct6").split()
    gpsimd = "pk send gn".split()
    between = {6: "xf3", 7: "ox3", 9: "xf4", 10: "ox4", 11: "li10", 12: "up10", 13: "xf5", 14: "ox5", 16: "qf10", 18: "xf6", 19: "ox6"}
    if w == 0:
        vector = "kv0 first li0 li2 li4 kv1 up0 qf0 cv0 kv2 cv1 S0 cv2 up2 qf2 xf0 ox0 s0 up4 xf1 s1 ox1 qf4 s2 up6 s3 xf2 qf6 ox2".split()
        scalar = ["fr", "up_0", "ks0", "ks3", "x0", "ks1", "xc0", "ks2"] + scalar[3:] + ["ks4"]
        tensor = ["xt0", "kp"] + tensor[8:]
        gpsimd = ["kg0", "send", "kg1", "gn"]
        between.update({4: "up8", 5: "qf8", 8: "kv8", 15: "kv3", 17: "kv4", 20: "kv5", 21: "kv6", 22: "kv7"})
    for c in range(4, 24):
        vector += ["s%d" % c, between.get(c)]
    return {"D": vector, "A": scalar, "P": tensor, "G": gpsimd, "S": ["load", "mo", "cd", "mi", "store"]}


SCRATCH = {
    "St0": ("sbuf", [128, WIN], "bfloat16"), "St1": ("sbuf", [128, WIN], "bfloat16"),
    "UPS": ("sbuf", [128, UPW], "int32"), "FR": ("sbuf", [128, 10], "int32"),
    "OG": ("sbuf", [128, 3072], "bfloat16"), "CM": ("sbuf", [128, 3072], "bfloat16"), "OF": ("sbuf", [128, 3072], "bfloat16"),
    "LF": ("sbuf", [128, 16], "float32"), "LP": ("sbuf", [128, 12], "uint16"), "PQ": ("sbuf", [128, 192], "uint16"),
    "QF": ("sbuf", [128, 192], "float32"), "XF": ("sbuf", [128, 192], "float32"), "OX": ("sbuf", [128, 192], "uint16"),
    "XS": ("sbuf", [128, RO * XW], "bfloat16"), "LAND": ("sbuf", [128, RO * D * SLOT], "bfloat16"),
    "XT": ("sbuf", [128, 128 * len(TILES)], "bfloat16"),
    "CC": ("sbuf", [128, 10 * PW], "bfloat16"), "PC": ("sbuf", [128, 10 * PW], "bfloat16"),
    "FL": ("sbuf", [128, 3 * PW], "bfloat16"), "RS": ("sbuf", [128, 6 * PW], "bfloat16"),
    "MK": ("sbuf", [128, 200], "bfloat16"), "MC": ("sbuf", [128, 200], "bfloat16"),
    "EI": ("sbuf", [128, 512], "bfloat16"), "SH": ("sbuf", [128, 384], "bfloat16"), "ES": ("sbuf", [128, 1536], "bfloat16"), "E1": ("sbuf", [128, 256], "bfloat16"),
    "II": ("sbuf", [128, 128], "bfloat16"), "ID": ("sbuf", [128, 128], "bfloat16"), "IZ": ("sbuf", [128, 128], "bfloat16"),
    "HB": ("sbuf", [128, 128 * (RO + 1)], "bfloat16"), "DP": ("sbuf", [128, 256], "bfloat16"),
    "TI": ("sbuf", [128, 32], "float32"), "TR": ("sbuf", [128, 32], "bfloat16"),
    "Z": ("sbuf", [128, 288], "bfloat16"), "T8": ("sbuf", [128, 16], "bfloat16"), "ONE": ("sbuf", [128, 512], "bfloat16"),
    "SI": ("sbuf", [128, 144], "bfloat16"), "SEL": ("sbuf", [128, 144 * (RO - 1)], "bfloat16"), "MAG": ("sbuf", [128, 128], "bfloat16"),
    "KI": ("sbuf", [128, 8], "int32"), "CF": ("sbuf", [128, 64], "float32"), "CB": ("sbuf", [128, 4], "bfloat16"),
}
for _i in range(8):
    SCRATCH["P%d" % _i] = ("psum", [128, 512], "float32")
SEMAPHORES = (["sP", "sA", "sD", "sG", "dfr", "drec0", "drec1", "dy", "dmo", "dmi", "snt"] + ["dup%d" % i for i in range(6)]
              + ["arr%d" % w for w in range(RO)] + ["dcp%d" % w for w in range(RO)])
ORDER = []


def is_psum(buf):
    return SCRATCH[buf][0] == "psum"


def order_of(calls):
    before, seen = [], {}
    for n, c in enumerate(calls):
        pre = set()
        for acc, wr in ((c[1], False), (c[2], True)):
            for buf, a, b in acc:
                pre.update(m for a0, b0, wr0, m in seen.get(buf, []) if is_psum(buf) or (a0 < b and b0 > a and (wr or wr0)))
        for acc, wr in ((c[1], False), (c[2], True)):
            for buf, a, b in acc:
                h = seen.setdefault(buf, [])
                if wr or is_psum(buf):
                    h[:] = [e for e in h if not (is_psum(buf) or (a <= e[0] and e[1] <= b))]
                h.append((a, b, wr, n))
        before.append(pre)
    lines = {}
    for w in range(RO):
        for q, steps in plan(w).items():
            lines.setdefault(q, []).extend(n for s in steps for n, c in enumerate(calls) if c[0] == q and c[3] == (w, s))
    order, done = [], set()
    while len(order) < len(calls):
        had = len(order)
        for line in lines.values():
            while line and before[line[0]] <= done:
                done.add(line[0])
                order.append(line.pop(0))
        assert len(order) > had, "the plan goes against the data flow"
    return order


def rank_program(g, core, T, topo):
    rank = T.rank_of(core)
    if rank is None:
        return
    queues = {"P": g.tensor, "A": g.scalar, "D": g.vector, "G": g, "S": g.sync}
    vec, act, ten = g.vector, g.scalar, g.tensor
    calls, now = [], [0, ""]

    def step(name, j=""):
        now[1] = "%s%s" % (name, j)

    def run(q, reads, writes, f, *args, **kw):
        calls.append((q, reads, writes, tuple(now), None, f, args, kw))

    def dma(q, sem, reads, writes, out, in_):
        calls.append((q, reads, writes, tuple(now), sem, queues[q].dma_start, (out, in_), {}))

    def ap(x, n=128, p0=0):
        if not isinstance(x, tuple):
            return x
        s = x[3] if len(x) > 3 else 1
        return T[x[0]][p0:p0 + n, x[1]:x[2]:s] if s != 1 else T[x[0]][p0:p0 + n, x[1]:x[2]]

    def rg(*xs):
        return [x[:3] for x in xs if isinstance(x, tuple)]

    def memset(x, c, n=128, p0=0):
        run("D", [], rg(x), vec.memset, ap(x, n, p0), c)

    def ts(out, in0, s1, s2, op0, op1=None, n=128):
        run("D", rg(in0, s1, s2), rg(out), vec.tensor_scalar, ap(out, n), ap(in0, n), ap(s1, n), ap(s2, n), *[o for o in (op0, op1) if o is not None])

    def tt(out, a, b, op):
        run("D", rg(a, b), rg(out), vec.tensor_tensor, ap(out), ap(a), ap(b), op)

    def cp(out, in_):
        run("D", rg(in_), rg(out), vec.tensor_copy, ap(out), ap(in_))

    def scan(out, d0, d1, first, op0, op1):
        run("D", rg(d0, d1, first), rg(out), vec.tensor_tensor_scan, ap(out), ap(d0), ap(d1), ap(first), op0, op1)

    def actv(out, in_, f=AF.Identity, bias=0.0, scale=1.0, n=128, p0=0):
        run("A", rg(in_, bias, scale), rg(out), act.activation, ap(out, n, p0), ap(in_, n, p0), f, bias=ap(bias), scale=ap(scale))

    def mm(out, lhsT, rhs, start, stop, m=128, k=128):
        run("P", rg(lhsT, rhs), rg(out), ten.matmul, ap(out, m), ap(lhsT, k), ap(rhs, k), start, stop)

    def iota(x, pat, base, cm, n=128):
        kw = {} if SCRATCH[x[0]][2] == "int32" else {"allow_small_or_imprecise_dtypes": True}
        run("G", [], rg(x), g.iota, ap(x, n), pat, base, cm, **kw)

    def sel(out, in_, pat, op, base, cm):
        run("G", rg(in_), rg(out), g.affine_select, ap(out), ap(in_), pat, op, 0.0, base, cm)

    def gcopy(out, in_):
        sel(out, in_, [[0, out[2] - out[1]]], OP.is_ge, 1, 0)

    def by(window, offsets):
        return ap(window).indirect(ap(offsets))

    step("fr")
    dma("A", "dfr", [], [("FR", 0, 10)], T.FR[:], T.fr[:])
    step("load")
    for j, (a, b) in enumerate(PIECES):
        dma("S", "drec%d" % j, [], [("St0", a, b)], T.St0[:, a:b], T.rec[:, a:b])
    for i in range(6):
        a = 640 * i if i < 5 else GH
        step("load" if i else "up_0")
        dma("S" if i else "A", "dup%d" % i, [], [("UPS", a, a + 640)], T.UPS[:, a:a + 640], T.up[:, 640 * i:640 * i + 640])

    C = {n: ("CF", j, j + 1) for j, n in enumerate(["p", "m0", "p160", "r", "scol", "nr", "t", "zs", "zb", "own", "ghost", "thr", "drop"])}
    HC = [("CF", 14 + w, 15 + w) for w in range(RO)]
    BASE, CAP, GB = ("CF", 36, 46), ("CB", 0, 1), ("CB", 2, 4)
    NT = 128 * len(TILES)

    def line(out, a, b):
        actv(out, C["r"], bias=float(a), scale=float(b - a))

    step("kg0")
    iota(("KI", 0, 1), [[0, 1]], 0, 1)
    iota(("CF", 20, 30), [[320, 10]], 0, 0)
    iota(("II", 0, 128), [[-1, 128]], 0, 1)
    iota(("EI", 0, 512), [[-1, 32], [0, 16]], 0, 1, n=96)
    iota(("TI", 0, 32), [[0, 4], [16, 8]], 0, 0)
    step("kv0")
    memset(("ONE", 0, 512), 1.0)
    memset(("XT", 0, NT), 0.0, n=96)
    ts(("KI", 1, 2), ("KI", 0, 1), 3, 1, OP.logical_shift_right, OP.bitwise_and)
    ts(("KI", 2, 3), ("KI", 0, 1), 7, None, OP.bitwise_and)
    ts(("KI", 3, 4), ("KI", 0, 1), 15, None, OP.bitwise_and)
    memset(("St0", V, SW), 0.0)
    ts(C["p160"], ("KI", 1, 2), 160.0, None, OP.mult)
    ts(C["r"], ("KI", 3, 4), 15.0, None, OP.is_equal)
    cp(C["p"], ("KI", 1, 2))
    cp(C["t"], ("KI", 3, 4))
    ts(("ID", 0, 128), ("II", 0, 128), 0.0, None, OP.is_equal)
    ts(BASE, ("CF", 20, 30), C["p160"], None, OP.add)
    memset(("XT", 0, NT), 1.0, n=1, p0=96)
    memset(("MAG", 0, 128), WHOLE, n=1)
    memset(("Z", 0, 288), 0.0)
    memset(("St1", V, SW), 0.0)
    memset(("XT", 15, NT, 16), 0.0, n=1, p0=96)
    memset(("MAG", 15, 128, 16), 0.0, n=1)
    step("kg0")
    sel(("T8", 0, 8), ("ONE", 0, 8), [[-16, 8]], OP.is_ge, 0, 1)
    sel(("T8", 8, 16), ("T8", 0, 8), [[16, 8]], OP.is_ge, 15, -1)
    step("ks0")
    actv(("ES", 0, 512), ("ONE", 0, 512), scale=-0.25, n=1, p0=96)
    line(C["scol"], 1, -1)
    line(C["nr"], 1, 0)
    line(C["drop"], -WHOLE, 1)
    line(C["zs"], -STEP, SHIFT)
    line(C["zb"], -2 * STEP, SHIFT + 15 * STEP)
    for w in range(RO):
        line(HC[w], 0.5, tag(w) if w < RO - 1 else 0.0)
    actv(("IZ", 0, 128), ("ID", 0, 128), scale=C["nr"])
    actv(("HB", 0, 128), ("ID", 0, 128), scale=-0.5)
    actv(("HB", 128, 256), ("ID", 0, 128), scale=HC[0])
    step("ks1")
    actv(("TR", 0, 32), ("TI", 0, 32), bias=C["t"])
    actv(("Z", 15, 128, 16), ("T8", 8, 16), scale=C["zs"])
    actv(("Z", 144 + 15, 144 + 128, 16), ("T8", 8, 16), scale=C["zb"])
    step("kv1")
    ts(("ES", 0, 512), ("EI", 0, 512), 0.0, 0.5, OP.is_equal, OP.mult, n=96)
    ts(("E1", 0, 256), ("EI", 0, 256), 0.0, None, OP.is_equal, n=96)
    for j in (1, 2):
        step("kv1")
        ts(("SH", 128 * j, 128 * j + 128), ("II", 0, 128), -32.0 * j, None, OP.is_equal, n=96)
        run("D", [("ID", 0, 128)], [("SH", 128 * j, 128 * j + 128)], vec.tensor_copy, T.SH[96:97, 128 * j:128 * j + 128], T.ID[96:97, 0:128])
        step("kp")
        mm(("P%d" % (4 + j), 0, 512), ("SH", 128 * j, 128 * j + 97), ("ES", 0, 512), True, True, m=97, k=97)
        step("ks2")
        actv(("ES", 512 * j, 512 * j + 512), ("P%d" % (4 + j), 0, 512), AF.Copy, n=97)
    step("ks3")
    line(CAP, 255, 1)
    actv(C["m0"], C["p"], bias=1.0, scale=-1.0)
    actv(GB, ("CF", 36, 38))
    actv(("DP", 0, 128), ("ID", 0, 128), scale=C["m0"])
    actv(("DP", 128, 256), ("ID", 0, 128), scale=C["p"])
    step("ks4")
    for w in range(1, RO):
        actv(("HB", 128 * w + 128, 128 * w + 256), ("ID", 0, 128), scale=HC[w])
    step("kv2")
    ts(C["own"], ("KI", 2, 3), float(V), None, OP.add)
    ts(C["ghost"], ("KI", 2, 3), float(D * B), None, OP.add)
    ts(C["thr"], ("KI", 2, 3), BIG, BIG, OP.mult, OP.add)
    memset(("RS", 0, 6 * PW), 0.0)
    step("kv8")
    memset(("RS", B, 6 * PW, PW), 2.0 ** 20)
    step("kg1")
    iota(("UPS", V, V + 16), [[16, 16]], V, 1)
    iota(("UPS", GH + D * B, UPW), [[16, 16]], V, 1)
    iota(("SI", 0, 144), [[-16, 9], [-1000, 2], [0, 8]], 985, 1)
    iota(("FL", 0, 3 * PW), [[0, 3], [1, PW]], 0, 0)
    for w in range(RO - 1):
        step("kv", 3 + w)
        ts(("SEL", 144 * w, 144 * w + 144), ("SI", 0, 144), 0.0, -BIG / tag(w), OP.is_equal, OP.mult)
    step("kv7")
    ts(("FL", B, 3 * PW, PW), ("ONE", 0, 3), C["thr"], None, OP.mult)

    dests = [T.cores[(rank + d) % 8] for d in range(1, D + 1)]
    pick, used = {}, set()
    for dst in sorted(dests, key=lambda c: len(topo.engines(core, c))):
        e = [x for x in topo.engines(core, dst) if x not in used][:2]
        used.update(e)
        pick[dst] = sum(1 << x for x in e)

    for w in range(RO):
        now[0] = w
        X, Y = "St%d" % (w % 2), "St%d" % ((w + 1) % 2)
        xs, land = XW * w, SLOT * D * w

        def notes(c0, c1):
            return ("XS", xs + 16 + 16 * c0, xs + 16 + 16 * c1)

        def parents(c0, c1, window):
            pq = ("PQ", 16 * c0, 16 * c1)
            step("up", c0)
            run("D", [("LP", c0, c1), window], [pq], vec.tensor_copy, ap(pq), by(window, ("LP", c0, c1)))
            step("qf", c0)
            cp(("QF", 16 * c0, 16 * c1), pq)

        def gather_x(c0, c1):
            step("x", c0)
            window = (X, 0, SW if w else 320 * c1)
            run("A", [("LP", c0, c1), window], [notes(c0, c1)], act.activation, ap(notes(c0, c1)), by(window, ("LP", c0, c1)), AF.Copy)

        cv, cs, cg = CFG["cv"], CFG["cs"], CFG["cg"]
        if w == 0:
            for j, (a, b) in enumerate(((0, 640), (640, 1600), (1600, V))):
                step("cv", j)
                cp((Y, a, b), (X, a, b))
        else:
            step("cv0")
            ts((Y, 0, cv), (X, 0, cv), CAP, None, OP.min)
            if w < RO - 1:
                a = cv + cs + cg
                step("cs")
                actv((Y, cv, cv + cs), (X, cv, cv + cs), AF.Copy)
                step("cd")
                dma("S", "dcp%d" % w, [(X, a, V)], [(Y, a, V)], T[Y][:, a:V], T[X][:, a:V])
            else:
                a = cv + cs // 2
                step("cs")
                actv(("OF", cv, a), (X, cv, a), AF.Relu, bias=C["r"], scale=C["scol"])
                actv((Y, cv, a), ("OF", cv, a), bias=C["r"], scale=C["scol"])
                n = (V - a) // 16
                step("mo")
                dma("S", "dmo", [(X, a, V)], [("MK", 0, n)], T.MK[:, 0:n], T[X][15:128:16, a:V])
                step("cd")
                for j in range(8):
                    dma("S", "dcp%d" % w, [(X, a, V)], [(Y, a + 16 * j, a + 16 * j + 16)], T[Y][16 * j:16 * j + 15, a:V], T[X][16 * j:16 * j + 15, a:V])
                step("cap")
                ts(("MC", 0, n), ("MK", 0, n), 1.0, None, OP.min)
                step("mi")
                dma("S", "dmi", [("MC", 0, n)], [(Y, a + 128, V)], T[Y][15:128:16, a:V], T.MC[:, 0:n])

        if w == 0:
            step("first")
            tt(("LF", 0, 10), ("FR", 0, 10), BASE, OP.add)
            cp(("XS", xs + 14, xs + 16), ("FR", 0, 2))
            for c0, c1 in LISTS:
                step("li", c0)
                cp(("LP", c0, c1), ("LF", c0, c1))
                gather_x(c0, c1)
                for c in range(c0, c1, 2):
                    parents(c, c + 2, ("UPS", 0, 320 * c + 640))
        else:
            for c0, c1, pb in SCANS:
                src = (pb, 0, PW * (c1 - c0))
                for c in range(c0, c1):
                    step("mk", c)
                    for p in (0, 1):
                        b, s = 2 * c + p, 144 * (w - 1) + 8 - 8 * p
                        mm((pb, PW * (c - c0), PW * (c - c0 + 1)), ("SEL", s, s + 128), (X, B * b, B * b + PW), p == 0, p == 1)
                step("rem", c0)
                scan(("CC", PW * c0, PW * c1), src, ("FL", 0, src[2]), C["thr"], OP.add, OP.max)
            for c0, c1 in LISTS:
                a, b = PW * c0, PW * c1
                for x, y in ((0, 1), (1, 2)) if c0 == 0 else ((c0, c1),):
                    step("pl", x)
                    scan(("PC", PW * x, PW * y), ("RS", 0, PW * (y - x)), ("CC", PW * x, PW * y), 2.0 ** 20, OP.add, OP.min)
                if c1 - c0 <= 2:
                    for c in range(c0, c1):
                        step("li", c)
                        ts(("LP", c, c + 1), ("PC", PW * c + B - 1, PW * c + B), ("CF", 36 + c, 37 + c), C["own"], OP.add, OP.min)
                else:
                    step("lf", c0)
                    tt(("LF", c0, c1), ("PC", a + B - 1, b, PW), ("CF", 36 + c0, 36 + c1), OP.add)
                    step("li", c0)
                    ts(("LP", c0, c1), ("LF", c0, c1), C["own"], None, OP.min)
                parents(c0, c1, ("UPS", 0, GH))
                gather_x(c0, c1)
            step("pk")
            run("G", [("PC", B - 1, 2 * PW)], [("XS", xs + 14, xs + 16)], g.affine_select, T.XS[:, xs + 14:xs + 16], T.PC[:, B - 1:2 * PW:PW],
                [[0, 2]], OP.is_ge, 0.0, 1, 0)

        step("send")
        calls.append(("G", [("XS", xs + 14, xs + 48)], [("LAND", land, land + SLOT * D)], tuple(now), "arr%d" % w, g.remote_dma_fused, ([RemoteDMATransfer(
            dst_ids=[DstId(rid=topo.addr(dst)[0], pnc=topo.addr(dst)[1])], dma_engine_mask=pick[dst], remote_sem=T.sem["arr%d" % w],
            src=T.XS[:, xs + 14:xs + 48], dst=T.LAND[:, land + SLOT * d + 14:land + SLOT * d + 48]) for d, dst in enumerate(dests)],),
            {"local_sem": T.sem.snt}))

        def ghosts():
            step("gn")
            for d in range(D):
                s = land + SLOT * d + 16 + 8 * d
                gcopy(("XS", xs + 176 + 8 * d, xs + 184 + 8 * d), ("LAND", s, s + 8))
            step("gp")
            for p in (0, 1):
                s = land + SLOT * p + 14
                mm(("P0", 384, 386), ("DP", 128 * p, 128 * p + 128), ("LAND", s, s + 2 * SLOT + 2, 2 * SLOT + 1), p == 0, False)
            mm(("P0", 384, 386), ("ID", 0, 128), GB, False, True)
            step("li", 10)
            ts(("LP", 10, 12), ("P0", 384, 386), C["ghost"], None, OP.min)
            parents(10, 12, ("UPS", GH, UPW))

        for i, (c0, c1) in enumerate(CHUNKS):
            j, (t0, t1, pb) = [(j, t) for j, t in enumerate(TILES) if t[0] <= c0 < t[1]][0]
            tile = ("XT", 128 * j, 128 * j + 128)
            if c0 == t0:
                if t1 > 10:
                    ghosts()
                step("xt", j)
                mm((pb, 0, 128), notes(t0, t1), ("IZ", 0, 128), True, True, m=16 * (t1 - t0))
                step("xc", j)
                actv(tile, (pb, 0, 128), AF.Copy, n=16 * (t1 - t0))
            n = 256 * (c1 - c0)
            og, cm, of = [(buf, 256 * c0, 256 * c1) for buf in ("OG", "CM", "OF")]
            pq, qf, xf, ox = [(buf, 16 * c0, 16 * c1) for buf in ("PQ", "QF", "XF", "OX")]
            pc, pd, ps = ("P%d" % (1 + i % 2), 0, n // 16), ("P%d" % (3 + i % 2), 0, n), ("P%d" % (5 + i % 2), 0, n)
            spread = ("ES", 256 * (c0 - t0), 256 * (c1 - t0))
            step("G", i)
            run("A", [pq, (X, 0, SW), C["scol"], C["r"]], [og],
                act.activation, ap(og), by((X, 0, SW), pq), AF.Relu, bias=ap(C["r"]), scale=ap(C["scol"]))
            step("dx", i)
            if i == 0:
                mm(pd, tile, ("E1", 0, n), True, True, k=96)
                step("S", i)
                tt(cm, og, pd, OP.is_ge)
            else:
                mm(pd, tile, spread, True, False, k=97)
                step("do", i)
                mm(pd, ("HB", 0, 128), og, False, True)
                step("S", i)
                actv(cm, pd, AF.Sign, bias=0.125, scale=-1.0)
            step("sx", i)
            mm(ps, tile, spread, True, False, k=97)
            step("so", i)
            mm(ps, ("HB", 128 * w + 128, 128 * w + 256), og, False, False)
            step("sm", i)
            mm(ps, ("MAG", 0, 128), ("ONE", 0, n), False, True, k=1)
            step("O", i)
            actv(of, ps, bias=C["drop"])
            step("op", i)
            mm(pc, ("ID", 0, 128), ("TR", 0, n // 16), True, False)
            step("ct", i)
            z = 144 * (i == 0)
            for t in range(16):
                mm(pc, ("Z", z + 15 - t, z + 143 - t), ("CM", cm[1] + t, cm[2], 16), False, t == 15)
            step("xf", i)
            tt(xf, pc, qf, OP.max)
            step("ox", i)
            cp(ox, xf)
            for c in range(2 * c0, 2 * c1):
                step("s", c)
                run("D", [("OX", 8 * c, 8 * c + 8), ("OF", 128 * c, 128 * c + 128)], [(Y, 0, WIN)],
                    vec.tensor_copy, by((Y, 0, WIN), ("OX", 8 * c, 8 * c + 8)), T.OF[:, 128 * c:128 * c + 128])

    step("store")
    dma("S", "dy", [("St%d" % (RO % 2), 0, V)], [], T.y[:], T["St%d" % (RO % 2)][:, 0:V])

    count = {"sP": 0, "sA": 0, "sD": 0, "sG": 0}
    whole = {}
    for c in calls:
        whole[c[4]] = whole.get(c[4], 0) + 16
    know = {q: {} for q in queues}
    hist = {}
    if not ORDER:
        ORDER.extend(order_of(calls))
    for n in ORDER:
        q, reads, writes, _, sem, f, args, kw = calls[n]
        remote = sem is not None and sem.startswith("arr")
        found = []
        for acc, wr in ((reads, False), ([] if remote else writes, True)):
            for buf, a, b in acc:
                for e in hist.get(buf, []):
                    if is_psum(buf):
                        if e[3] != q:
                            found.append(e)
                    elif e[0] < b and e[1] > a and (e[2] or (wr and e[3] != q)):
                        found.append(e)
        k, best = know[q], {}
        for e in found:
            if k.get(e[4], 0) >= e[5] or any(o is not e and o[6].get(e[4], 0) >= e[5] for o in found):
                continue
            best[e[4]] = max(best.get(e[4], 0), e[5])
        for s, v in best.items():
            queues[q].wait_ge(T.sem[s], v)
        for e in found:
            k[e[4]] = max(k.get(e[4], 0), e[5])
            for s, v in e[6].items():
                k[s] = max(k.get(s, 0), v)
        snap = dict(k)
        if remote:
            f(*args, **kw)
            who, value, reads, snap = "remote", 2 * D, [], {}
        elif sem:
            f(*args, **kw).then_inc(T.sem[sem], 16)
            who, value = sem, whole[sem]
            count[sem] = value
        else:
            sem = "s" + q
            f(*args, **kw).then_inc(T.sem[sem], 1)
            count[sem] += 1
            who, value = q, count[sem]
        for acc, wr in ((reads, False), (writes, True)):
            for buf, a, b in acc:
                h = hist.setdefault(buf, [])
                h[:] = [e for e in h if not (a <= e[0] and e[1] <= b and (wr or (not e[2] and e[3] == who)))]
                h.append((a, b, wr, who, sem, value, snap))
    for s, v in count.items():
        g.wait_ge(T.sem[s], v)
    g.wait_ge(T.sem.snt, 2 * D * RO)
